import numpy as np
import ml_dtypes


def mxq(x, axis, fmt="e4m3"):
    dtype, down = {"e4m3": (ml_dtypes.float8_e4m3fn, 7), "e5m2": (ml_dtypes.float8_e5m2, 14)}[fmt]
    v = np.moveaxis(np.asarray(x, np.float32).astype(ml_dtypes.bfloat16).astype(np.float64), axis, -1)
    blocks = v.reshape(v.shape[:-1] + (-1, 32))
    amax = np.abs(blocks).max(-1, keepdims=True)
    byte = np.maximum(np.where(amax > 0, np.frexp(amax)[1] - 1 + 127, 0) - down, 1)
    scale = np.exp2(byte - 127.0)
    codes = (blocks / scale).astype(np.float32).astype(dtype).astype(np.float64)
    return np.moveaxis((codes * scale).reshape(v.shape), -1, axis)


WIDE = False


def mx_kscale(k):
    if not WIDE:
        return np.ones(k)
    levels = np.array([10, -10, 5, -5, 0])
    if k % 512:
        return np.exp2(np.random.permutation(np.resize(levels, k // 32))).repeat(32)
    a = np.empty((k // 512, 16))
    for p in range(k // 512):
        a[p, :8] = np.random.permutation(np.resize(levels, 8))
        for g in range(8):
            far = levels[np.abs(levels - a[p, g]) >= 10]
            a[p, g + 8] = far[np.random.randint(len(far))]
    return np.exp2(a.ravel()).repeat(32)


def f64(x):
    return np.asarray(x).astype(np.float64)


def striped(idx):
    return np.tile(idx.reshape(-1, 16).T, (8, 1)).astype(np.uint16)


def unstriped(offs):
    return offs[:16].T.reshape(-1).astype(np.int64)


def pack_weight(w):
    k, n = w.shape
    w = f64(np.asarray(w, np.float32).astype(ml_dtypes.bfloat16)).reshape(k // 32, 32, n)
    amax = np.abs(w).max(1)
    byte = np.clip(np.where(amax > 0, np.frexp(amax)[1] - 1 + 127 - 7, 1), 1, 254)
    scaled = (w * np.exp2(127.0 - byte)[:, None, :]).reshape(k, n).astype(np.float32)
    words = np.ascontiguousarray(scaled.reshape(k // 512, 128, 4, n).transpose(0, 1, 3, 2)).astype(ml_dtypes.float8_e4m3fn).view(np.uint8)
    return words, np.ascontiguousarray(byte.astype(np.uint8).reshape(k // 512, 16, n))


def unpack_weight(words, scales):
    g, p, n, _ = words.shape
    vals = np.ascontiguousarray(words).view(ml_dtypes.float8_e4m3fn).astype(np.float64) * np.repeat(np.exp2(scales.astype(np.float64) - 127.0), 8, axis=1)[..., None]
    return vals.transpose(0, 1, 3, 2).reshape(g * 512, n)


def relu(v):
    return np.maximum(v, 0.0)

def planes(y):
    n, m = y.shape
    v = y.astype(np.float32).astype(ml_dtypes.bfloat16).astype(np.float64).reshape(n // 32, 32, m)
    top = np.abs(v).max(1)
    byte = np.clip(np.where(top > 0, np.frexp(top)[1] - 1 + 127 - 7, 1), 1, 254)
    codes = (v * np.exp2(127.0 - byte)[:, None, :]).reshape(n, m).astype(np.float32).astype(ml_dtypes.float8_e4m3fn).view(np.uint8)
    words = codes.reshape(n // 512, 128, 4, m).transpose(0, 1, 3, 2)
    return np.ascontiguousarray(words), np.ascontiguousarray(byte.astype(np.uint8).reshape(n // 512, 16, m))


K, T, S, N, U = 512, 2048, 1024, 512, 2048


def setup_inputs():
    n = np.random.standard_normal
    s = mx_kscale(K)[:, None]
    packed_xT = pack_weight(n((K, T)) * s)
    return {
        "x_words": packed_xT[0],
        "x_scales": packed_xT[1],
        "w1": (n((K, N)) / np.sqrt(K) / s).astype(np.float32),
        "res": n((N, U)).astype(np.float32),
        "offs": striped(np.random.permutation(T)[:S]),
        "own": striped(np.random.randint(0, S, U)),
    }


def reference(x_words, x_scales, w1, res, offs, own):
    xq = unpack_weight(x_words, x_scales)[:, unstriped(offs)]
    y = relu(mxq(f64(w1), 0, "e4m3").T @ xq)
    out_0 = f64(res) + y[:, unstriped(own)]
    return (out_0,) + planes(out_0)

@@ -1,0 +1,143 @@
+from contextlib import ExitStack
+
+import concourse.mybir as mybir
+
+K, T, S, N, U = 512, 2048, 1024, 512, 2048
+FLOPS = 2 * K * N * S
+
+F32 = mybir.dt.float32
+BF16 = mybir.dt.bfloat16
+I32 = mybir.dt.int32
+U32 = mybir.dt.uint32
+U16 = mybir.dt.uint16
+U8 = mybir.dt.uint8
+FP8X4 = mybir.dt.float8_e4m3fn_x4
+ADD = mybir.AluOpType.add
+RELU = mybir.ActivationFunctionType.Relu
+
+P = 128
+PACK = 4
+BANK = 512
+STRIPE = 16
+STRETCH = 512
+PIECES = [(0, 512), (512, 512), (1024, 512), (1536, 256), (1792, 128), (1920, 128)]
+
+
+def tile_picked_unmerge_relu_po_kernel(tc, x_words, x_scales, w1, res, offs, own, out_0, out_1, out_2):
+    nc = tc.nc
+    with ExitStack() as ctx:
+        keep = ctx.enter_context(tc.tile_pool(name="keep", bufs=1))
+        psum = ctx.enter_context(tc.psum_pool(name="psum", bufs=1))
+
+        offs_sb = keep.tile([P, S // STRIPE], U16, name="offs_sb")
+        own_sb = keep.tile([P, U // STRIPE], U16, name="own_sb")
+        scale_table = keep.tile([P, T], U8, name="scale_table", align_bytes=64)
+        word_table = keep.tile([P, T], I32, name="word_table", align_bytes=64)
+        w_raw = keep.tile([P, PACK, N], F32, name="w_raw")
+
+        nc.vector.memset(scale_table[:].bitcast(I32), 0)
+        nc.sync.dma_start(offs_sb[:], offs)
+        for q in range(4):
+            nc.scalar.dma_start(
+                scale_table[32 * q : 32 * q + 4, :].bitcast(I32),
+                x_scales[0, 4 * q : 4 * q + 4, :].bitcast(I32),
+            )
+        nc.sync.dma_start(word_table[:], x_words[0].rearrange("p n t -> p (n t)").bitcast(I32))
+        nc.sync.dma_start(w_raw[:], w1.rearrange("(p j) c -> p j c", j=PACK))
+        nc.sync.dma_start(own_sb[:], own)
+        res_rows = res.rearrange("(p t) c -> p t c", t=PACK)
+        out_rows = out_0.rearrange("(p t) c -> p t c", t=PACK)
+        res_sb = []
+        for s in range(U // STRETCH):
+            r = keep.tile([P, PACK, STRETCH], F32, name=f"res{s}")
+            cols = slice(s * STRETCH, (s + 1) * STRETCH)
+            if s == 0:
+                for u in range(2):
+                    nc.sync.dma_start(r[:, 2 * u : 2 * u + 2, :], res_rows[:, 2 * u : 2 * u + 2, cols])
+            else:
+                nc.sync.dma_start(r[:], res_rows[:, :, cols])
+            res_sb.append(r)
+
+        x_scale = []
+        x_code = []
+        for h in range(S // BANK):
+            g = keep.tile([P, BANK], U8, name=f"x_scale{h}", align_bytes=64)
+            nc.vector.tensor_copy(g[:], scale_table[:].indirect(offs_sb[:, h * 32 : (h + 1) * 32]))
+            x_scale.append(g)
+        for h in range(S // BANK):
+            g = keep.tile([P, BANK], U32, name=f"x_code{h}", align_bytes=64)
+            nc.vector.tensor_copy(g[:], word_table[:].bitcast(U32).indirect(offs_sb[:, h * 32 : (h + 1) * 32]))
+            x_code.append(g)
+
+        w_src = w_raw[:].rearrange("p j (m t) -> p m j t", t=PACK)
+        w_code = []
+        w_scale = []
+        w_bf = []
+        for u in range(2):
+            wb = keep.tile([P, 2, P, PACK], BF16, name=f"w_bf{u}", align_bytes=64)
+            dst = wb[:].rearrange("p t m j -> p m j t")
+            if u == 0:
+                nc.scalar.copy(dst, w_src[:, :, :, 0:2])
+            else:
+                nc.vector.tensor_copy(dst, w_src[:, :, :, 2:4])
+            w_bf.append(wb)
+        for t in range(PACK):
+            c = keep.tile([P, P], U32, name=f"w_code{t}", align_bytes=64)
+            sc = keep.tile([P, P], U8, name=f"w_scale{t}", align_bytes=64)
+            nc.vector.quantize_mx(
+                out=c[:].bitcast(FP8X4),
+                scales=sc[:],
+                in_=w_bf[t // 2][:, t % 2, :, :].rearrange("p m j -> p (m j)"),
+            )
+            w_code.append(c)
+            w_scale.append(sc)
+
+        y = []
+        for t in range(PACK):
+            yt = keep.tile([P, S], F32, name=f"y{t}")
+            for h in range(S // BANK):
+                acc = psum.tile([P, BANK], F32, name=f"acc{t}_{h}")
+                nc.tensor.matmul_mx(
+                    out=acc[:],
+                    lhsT=w_code[t][:].bitcast(FP8X4),
+                    lhsT_scale=w_scale[t][:],
+                    rhs=x_code[h][:].bitcast(FP8X4),
+                    rhs_scale=x_scale[h][:],
+                    start=True,
+                    stop=True,
+                )
+                nc.scalar.activation(yt[:, h * BANK : (h + 1) * BANK], acc[:], RELU)
+            y.append(yt)
+
+        o_scale = keep.tile([P, STRETCH], U8, name="o_scale", align_bytes=64)
+        words_dram = out_1[0].rearrange("p n t -> p (n t)")
+        for i, (c0, n) in enumerate(PIECES):
+            s, o = divmod(c0, STRETCH)
+            summed = keep.tile([P, PACK, n], F32, name=f"summed{i}")
+            for t in range(PACK):
+                nc.vector.tensor_tensor(
+                    summed[:, t, :],
+                    y[t][:].indirect(own_sb[:, c0 // STRIPE : (c0 + n) // STRIPE]),
+                    res_sb[s][:, t, o : o + n],
+                    ADD,
+                )
+            nc.sync.dma_start(out_rows[:, :, c0 : c0 + n], summed[:])
+            rounded = keep.tile([P, n, PACK], BF16, name=f"rounded{i}", align_bytes=64)
+            nc.scalar.copy(
+                rounded[:].rearrange("p (c i) t -> p c t i", i=4),
+                summed[:].rearrange("p t (c i) -> p c t i", i=4),
+            )
+            o_code = keep.tile([P, n], U32, name=f"o_code{i}", align_bytes=64)
+            nc.vector.quantize_mx(
+                out=o_code[:].bitcast(FP8X4),
+                scales=o_scale[4 * s : P, o : o + n],
+                in_=rounded[:].rearrange("p n t -> p (n t)"),
+            )
+            nc.sync.dma_start(words_dram[:, 4 * c0 : 4 * (c0 + n)].bitcast(I32), o_code[:].bitcast(I32))
+        scales_dram = out_2[0].rearrange("r (s c) -> s r c", c=STRETCH)
+        for q in range(4):
+            eng = nc.sync if q % 2 == 0 else nc.scalar
+            eng.dma_start(
+                scales_dram[:, 4 * q : 4 * q + 4, :].bitcast(I32),
+                o_scale[32 * q : 32 * q + 16, :].bitcast(I32),
+            )

@@ -37,12 +37,14 @@ def tile_picked_unmerge_relu_po_kernel(tc, x_words, x_scales, w1, res, offs, own
 
         nc.vector.memset(scale_table[:].bitcast(I32), 0)
         nc.sync.dma_start(offs_sb[:], offs)
+        words_in = x_words[0].rearrange("p n t -> p (n t)").bitcast(I32)
+        nc.sync.dma_start(word_table[:, 0:512], words_in[:, 0:512])
         for q in range(4):
-            nc.scalar.dma_start(
+            nc.sync.dma_start(
                 scale_table[32 * q : 32 * q + 4, :].bitcast(I32),
                 x_scales[0, 4 * q : 4 * q + 4, :].bitcast(I32),
             )
-        nc.sync.dma_start(word_table[:], x_words[0].rearrange("p n t -> p (n t)").bitcast(I32))
+        nc.sync.dma_start(word_table[:, 512:T], words_in[:, 512:T])
         nc.sync.dma_start(w_raw[:], w1.rearrange("(p j) c -> p j c", j=PACK))
         nc.sync.dma_start(own_sb[:], own)
         res_rows = res.rearrange("(p t) c -> p t c", t=PACK)
@@ -51,11 +53,7 @@ def tile_picked_unmerge_relu_po_kernel(tc, x_words, x_scales, w1, res, offs, own
         for s in range(U // STRETCH):
             r = keep.tile([P, PACK, STRETCH], F32, name=f"res{s}")
             cols = slice(s * STRETCH, (s + 1) * STRETCH)
-            if s == 0:
-                for u in range(2):
-                    nc.sync.dma_start(r[:, 2 * u : 2 * u + 2, :], res_rows[:, 2 * u : 2 * u + 2, cols])
-            else:
-                nc.sync.dma_start(r[:], res_rows[:, :, cols])
+            nc.sync.dma_start(r[:], res_rows[:, :, cols])
             res_sb.append(r)
 
         x_scale = []
@@ -72,25 +70,24 @@ def tile_picked_unmerge_relu_po_kernel(tc, x_words, x_scales, w1, res, offs, own
         w_src = w_raw[:].rearrange("p j (m t) -> p m j t", t=PACK)
         w_code = []
         w_scale = []
-        w_bf = []
         for u in range(2):
-            wb = keep.tile([P, 2, P, PACK], BF16, name=f"w_bf{u}", align_bytes=64)
+            wb = keep.tile([P, 2, P, PACK], BF16, name=f"w_bf{u}", tag="w_bf", align_bytes=64)
             dst = wb[:].rearrange("p t m j -> p m j t")
             if u == 0:
                 nc.scalar.copy(dst, w_src[:, :, :, 0:2])
             else:
                 nc.vector.tensor_copy(dst, w_src[:, :, :, 2:4])
-            w_bf.append(wb)
-        for t in range(PACK):
-            c = keep.tile([P, P], U32, name=f"w_code{t}", align_bytes=64)
-            sc = keep.tile([P, P], U8, name=f"w_scale{t}", align_bytes=64)
-            nc.vector.quantize_mx(
-                out=c[:].bitcast(FP8X4),
-                scales=sc[:],
-                in_=w_bf[t // 2][:, t % 2, :, :].rearrange("p m j -> p (m j)"),
-            )
-            w_code.append(c)
-            w_scale.append(sc)
+            for e in range(2):
+                t = 2 * u + e
+                c = keep.tile([P, P], U32, name=f"w_code{t}", align_bytes=64)
+                sc = keep.tile([P, P], U8, name=f"w_scale{t}", align_bytes=64)
+                nc.vector.quantize_mx(
+                    out=c[:].bitcast(FP8X4),
+                    scales=sc[:],
+                    in_=wb[:, e, :, :].rearrange("p m j -> p (m j)"),
+                )
+                w_code.append(c)
+                w_scale.append(sc)
 
         y = []
         for t in range(PACK):
@@ -111,9 +108,11 @@ def tile_picked_unmerge_relu_po_kernel(tc, x_words, x_scales, w1, res, offs, own
 
         o_scale = keep.tile([P, STRETCH], U8, name="o_scale", align_bytes=64)
         words_dram = out_1[0].rearrange("p n t -> p (n t)")
+        o_code = [keep.tile([P, STRETCH], U32, name=f"o_code{s}", align_bytes=64) for s in range(U // STRETCH)]
+        last = len(PIECES) - 1
         for i, (c0, n) in enumerate(PIECES):
             s, o = divmod(c0, STRETCH)
-            summed = keep.tile([P, PACK, n], F32, name=f"summed{i}")
+            summed = keep.tile([P, PACK, n], F32, name=f"summed{i}", tag="shared" if i == last else f"summed{i}", align_bytes=64)
             for t in range(PACK):
                 nc.vector.tensor_tensor(
                     summed[:, t, :],
@@ -121,19 +120,24 @@ def tile_picked_unmerge_relu_po_kernel(tc, x_words, x_scales, w1, res, offs, own
                     res_sb[s][:, t, o : o + n],
                     ADD,
                 )
-            nc.sync.dma_start(out_rows[:, :, c0 : c0 + n], summed[:])
-            rounded = keep.tile([P, n, PACK], BF16, name=f"rounded{i}", align_bytes=64)
+                if i < 2 and t % 2 == 1:
+                    nc.sync.dma_start(out_rows[:, t - 1 : t + 1, c0 : c0 + n], summed[:, t - 1 : t + 1, :])
+            if i >= 2:
+                nc.sync.dma_start(out_rows[:, :, c0 : c0 + n], summed[:])
+            rounded = keep.tile([P, n, PACK], BF16, name=f"rounded{i}", tag="shared" if i == 2 else f"rounded{i}", align_bytes=64)
             nc.scalar.copy(
                 rounded[:].rearrange("p (c i) t -> p c t i", i=4),
                 summed[:].rearrange("p t (c i) -> p c t i", i=4),
             )
-            o_code = keep.tile([P, n], U32, name=f"o_code{i}", align_bytes=64)
             nc.vector.quantize_mx(
-                out=o_code[:].bitcast(FP8X4),
+                out=o_code[s][:, o : o + n].bitcast(FP8X4),
                 scales=o_scale[4 * s : P, o : o + n],
                 in_=rounded[:].rearrange("p n t -> p (n t)"),
             )
-            nc.sync.dma_start(words_dram[:, 4 * c0 : 4 * (c0 + n)].bitcast(I32), o_code[:].bitcast(I32))
+            if o + n == STRETCH:
+                nc.sync.dma_start(
+                    words_dram[:, 4 * s * STRETCH : 4 * (s + 1) * STRETCH].bitcast(I32), o_code[s][:].bitcast(I32)
+                )
         scales_dram = out_2[0].rearrange("r (s c) -> s r c", c=STRETCH)
         for q in range(4):
             eng = nc.sync if q % 2 == 0 else nc.scalar

@@ -20,7 +20,11 @@ PACK = 4
 BANK = 512
 STRIPE = 16
 STRETCH = 512
-PIECES = [(0, 512), (512, 512), (1024, 512), (1536, 256), (1792, 128), (1920, 128)]
+HALF = N // 2
+FIRST_WORDS = 512
+PIECES = [(0, 768), (768, 768), (1536, 384), (1920, 128)]
+RUNS = [(0, 512), (512, 512), (1024, 512), (1536, 256), (1792, 128), (1920, 128)]
+WORDS_AFTER = {1: (0,), 2: (1,), 3: (2, 3)}
 
 
 def tile_picked_unmerge_relu_po_kernel(tc, x_words, x_scales, w1, res, offs, own, out_0, out_1, out_2):
@@ -33,61 +37,56 @@ def tile_picked_unmerge_relu_po_kernel(tc, x_words, x_scales, w1, res, offs, own
         own_sb = keep.tile([P, U // STRIPE], U16, name="own_sb")
         scale_table = keep.tile([P, T], U8, name="scale_table", align_bytes=64)
         word_table = keep.tile([P, T], I32, name="word_table", align_bytes=64)
-        w_raw = keep.tile([P, PACK, N], F32, name="w_raw")
+        w_raw = [keep.tile([P, PACK, HALF], F32, name=f"w_raw{v}") for v in range(2)]
 
         nc.vector.memset(scale_table[:].bitcast(I32), 0)
         nc.sync.dma_start(offs_sb[:], offs)
         words_in = x_words[0].rearrange("p n t -> p (n t)").bitcast(I32)
-        nc.sync.dma_start(word_table[:, 0:512], words_in[:, 0:512])
+        nc.sync.dma_start(word_table[:, 0:FIRST_WORDS], words_in[:, 0:FIRST_WORDS])
         for q in range(4):
             nc.sync.dma_start(
                 scale_table[32 * q : 32 * q + 4, :].bitcast(I32),
                 x_scales[0, 4 * q : 4 * q + 4, :].bitcast(I32),
             )
-        nc.sync.dma_start(word_table[:, 512:T], words_in[:, 512:T])
-        nc.sync.dma_start(w_raw[:], w1.rearrange("(p j) c -> p j c", j=PACK))
+        nc.sync.dma_start(word_table[:, FIRST_WORDS:T], words_in[:, FIRST_WORDS:T])
+        w_rows = w1.rearrange("(p j) c -> p j c", j=PACK)
+        for v in range(2):
+            nc.sync.dma_start(w_raw[v][:], w_rows[:, :, v * HALF : (v + 1) * HALF])
         nc.sync.dma_start(own_sb[:], own)
         res_rows = res.rearrange("(p t) c -> p t c", t=PACK)
         out_rows = out_0.rearrange("(p t) c -> p t c", t=PACK)
         res_sb = []
-        for s in range(U // STRETCH):
-            r = keep.tile([P, PACK, STRETCH], F32, name=f"res{s}")
-            cols = slice(s * STRETCH, (s + 1) * STRETCH)
-            nc.sync.dma_start(r[:], res_rows[:, :, cols])
-            res_sb.append(r)
+        for i, (c0, n) in enumerate(PIECES):
+            rows = []
+            group = 2 if i == 0 else PACK
+            for t0 in range(0, PACK, group):
+                r = keep.tile([P, group, n], F32, name=f"res{i}_{t0}", tag=f"res{i}_{t0}", align_bytes=64)
+                nc.sync.dma_start(r[:], res_rows[:, t0 : t0 + group, c0 : c0 + n])
+                rows.extend([r[:, e, :] for e in range(group)])
+            res_sb.append(rows)
 
-        x_scale = []
-        x_code = []
-        for h in range(S // BANK):
-            g = keep.tile([P, BANK], U8, name=f"x_scale{h}", align_bytes=64)
-            nc.vector.tensor_copy(g[:], scale_table[:].indirect(offs_sb[:, h * 32 : (h + 1) * 32]))
-            x_scale.append(g)
-        for h in range(S // BANK):
-            g = keep.tile([P, BANK], U32, name=f"x_code{h}", align_bytes=64)
-            nc.vector.tensor_copy(g[:], word_table[:].bitcast(U32).indirect(offs_sb[:, h * 32 : (h + 1) * 32]))
-            x_code.append(g)
+        x_scale = keep.tile([P, S], U8, name="x_scale", align_bytes=64)
+        x_code = keep.tile([P, S], U32, name="x_code", align_bytes=64)
+        nc.vector.tensor_copy(x_scale[:], scale_table[:].indirect(offs_sb[:]))
+        nc.vector.tensor_copy(x_code[:], word_table[:].bitcast(U32).indirect(offs_sb[:]))
 
-        w_src = w_raw[:].rearrange("p j (m t) -> p m j t", t=PACK)
+        w_src = [w_raw[v][:].rearrange("p j (m t) -> p m j t", t=PACK) for v in range(2)]
+        w_bf = keep.tile([P, PACK, P, PACK], BF16, name="w_bf", align_bytes=64)
+        w_dst = w_bf[:].rearrange("p t m j -> p m j t")
+        for v, t0, t1 in ((0, 0, 4), (1, 0, 2), (1, 2, 4)):
+            nc.scalar.copy(w_dst[:, v * 64 : (v + 1) * 64, :, t0:t1], w_src[v][:, :, :, t0:t1])
         w_code = []
         w_scale = []
-        for u in range(2):
-            wb = keep.tile([P, 2, P, PACK], BF16, name=f"w_bf{u}", tag="w_bf", align_bytes=64)
-            dst = wb[:].rearrange("p t m j -> p m j t")
-            if u == 0:
-                nc.scalar.copy(dst, w_src[:, :, :, 0:2])
-            else:
-                nc.vector.tensor_copy(dst, w_src[:, :, :, 2:4])
-            for e in range(2):
-                t = 2 * u + e
-                c = keep.tile([P, P], U32, name=f"w_code{t}", align_bytes=64)
-                sc = keep.tile([P, P], U8, name=f"w_scale{t}", align_bytes=64)
-                nc.vector.quantize_mx(
-                    out=c[:].bitcast(FP8X4),
-                    scales=sc[:],
-                    in_=wb[:, e, :, :].rearrange("p m j -> p (m j)"),
-                )
-                w_code.append(c)
-                w_scale.append(sc)
+        for t in range(PACK):
+            c = keep.tile([P, P], U32, name=f"w_code{t}", align_bytes=64)
+            sc = keep.tile([P, P], U8, name=f"w_scale{t}", align_bytes=64)
+            nc.vector.quantize_mx(
+                out=c[:].bitcast(FP8X4),
+                scales=sc[:],
+                in_=w_bf[:, t, :, :].rearrange("p m j -> p (m j)"),
+            )
+            w_code.append(c)
+            w_scale.append(sc)
 
         y = []
         for t in range(PACK):
@@ -98,50 +97,56 @@ def tile_picked_unmerge_relu_po_kernel(tc, x_words, x_scales, w1, res, offs, own
                     out=acc[:],
                     lhsT=w_code[t][:].bitcast(FP8X4),
                     lhsT_scale=w_scale[t][:],
-                    rhs=x_code[h][:].bitcast(FP8X4),
-                    rhs_scale=x_scale[h][:],
+                    rhs=x_code[:, h * BANK : (h + 1) * BANK].bitcast(FP8X4),
+                    rhs_scale=x_scale[:, h * BANK : (h + 1) * BANK],
                     start=True,
                     stop=True,
                 )
-                nc.scalar.activation(yt[:, h * BANK : (h + 1) * BANK], acc[:], RELU)
+                if (t, h) == (0, 1):
+                    nc.vector.tensor_scalar_max(yt[:, h * BANK : (h + 1) * BANK], acc[:], 0.0)
+                else:
+                    nc.scalar.activation(yt[:, h * BANK : (h + 1) * BANK], acc[:], RELU)
             y.append(yt)
 
         o_scale = keep.tile([P, STRETCH], U8, name="o_scale", align_bytes=64)
-        words_dram = out_1[0].rearrange("p n t -> p (n t)")
         o_code = [keep.tile([P, STRETCH], U32, name=f"o_code{s}", align_bytes=64) for s in range(U // STRETCH)]
-        last = len(PIECES) - 1
+        rounded = [keep.tile([P, n, PACK], BF16, name=f"rounded{c0}", align_bytes=64) for c0, n in RUNS]
+        words_dram = out_1[0].rearrange("p n t -> p (n t)")
         for i, (c0, n) in enumerate(PIECES):
-            s, o = divmod(c0, STRETCH)
-            summed = keep.tile([P, PACK, n], F32, name=f"summed{i}", tag="shared" if i == last else f"summed{i}", align_bytes=64)
+            summed = keep.tile([P, PACK, n], F32, name=f"summed{i}", tag=f"summed{i}", align_bytes=64)
+            group = 2 if n >= STRETCH else PACK
             for t in range(PACK):
                 nc.vector.tensor_tensor(
                     summed[:, t, :],
                     y[t][:].indirect(own_sb[:, c0 // STRIPE : (c0 + n) // STRIPE]),
-                    res_sb[s][:, t, o : o + n],
+                    res_sb[i][t],
                     ADD,
                 )
-                if i < 2 and t % 2 == 1:
-                    nc.sync.dma_start(out_rows[:, t - 1 : t + 1, c0 : c0 + n], summed[:, t - 1 : t + 1, :])
-            if i >= 2:
-                nc.sync.dma_start(out_rows[:, :, c0 : c0 + n], summed[:])
-            rounded = keep.tile([P, n, PACK], BF16, name=f"rounded{i}", tag="shared" if i == 2 else f"rounded{i}", align_bytes=64)
-            nc.scalar.copy(
-                rounded[:].rearrange("p (c i) t -> p c t i", i=4),
-                summed[:].rearrange("p t (c i) -> p c t i", i=4),
-            )
-            nc.vector.quantize_mx(
-                out=o_code[s][:, o : o + n].bitcast(FP8X4),
-                scales=o_scale[4 * s : P, o : o + n],
-                in_=rounded[:].rearrange("p n t -> p (n t)"),
-            )
-            if o + n == STRETCH:
+                if (t + 1) % group == 0:
+                    rows = slice(t + 1 - group, t + 1)
+                    nc.sync.dma_start(out_rows[:, rows, c0 : c0 + n], summed[:, rows, :])
+            for (r0, m), run in zip(RUNS, rounded):
+                lo, hi = max(r0, c0), min(r0 + m, c0 + n)
+                if lo >= hi:
+                    continue
+                nc.scalar.copy(
+                    run[:, lo - r0 : hi - r0, :].rearrange("p (c i) t -> p c t i", i=4),
+                    summed[:, :, lo - c0 : hi - c0].rearrange("p t (c i) -> p c t i", i=4),
+                )
+                if hi == r0 + m:
+                    s, o = divmod(r0, STRETCH)
+                    nc.vector.quantize_mx(
+                        out=o_code[s][:, o : o + m].bitcast(FP8X4),
+                        scales=o_scale[4 * s : P, o : o + m],
+                        in_=run[:].rearrange("p n t -> p (n t)"),
+                    )
+            for z in WORDS_AFTER.get(i, ()):
                 nc.sync.dma_start(
-                    words_dram[:, 4 * s * STRETCH : 4 * (s + 1) * STRETCH].bitcast(I32), o_code[s][:].bitcast(I32)
+                    words_dram[:, 4 * z * STRETCH : 4 * (z + 1) * STRETCH].bitcast(I32), o_code[z][:].bitcast(I32)
                 )
         scales_dram = out_2[0].rearrange("r (s c) -> s r c", c=STRETCH)
         for q in range(4):
-            eng = nc.sync if q % 2 == 0 else nc.scalar
-            eng.dma_start(
+            nc.sync.dma_start(
                 scales_dram[:, 4 * q : 4 * q + 4, :].bitcast(I32),
                 o_scale[32 * q : 32 * q + 16, :].bitcast(I32),
             )

@@ -17,14 +17,18 @@ RELU = mybir.ActivationFunctionType.Relu
 
 P = 128
 PACK = 4
+PAIR = 2
+QUADRANT = 32
 BANK = 512
 STRIPE = 16
-STRETCH = 512
+LINE = 4
 HALF = N // 2
 FIRST_WORDS = 512
+STRETCH = 512
+
 PIECES = [(0, 768), (768, 768), (1536, 384), (1920, 128)]
 RUNS = [(0, 512), (512, 512), (1024, 512), (1536, 256), (1792, 128), (1920, 128)]
-WORDS_AFTER = {1: (0,), 2: (1,), 3: (2, 3)}
+WEIGHT_COPIES = [(0, 0, PACK), (1, 0, PAIR), (1, PAIR, PACK)]
 
 
 def tile_picked_unmerge_relu_po_kernel(tc, x_words, x_scales, w1, res, offs, own, out_0, out_1, out_2):
@@ -37,84 +41,87 @@ def tile_picked_unmerge_relu_po_kernel(tc, x_words, x_scales, w1, res, offs, own
         own_sb = keep.tile([P, U // STRIPE], U16, name="own_sb")
         scale_table = keep.tile([P, T], U8, name="scale_table", align_bytes=64)
         word_table = keep.tile([P, T], I32, name="word_table", align_bytes=64)
-        w_raw = [keep.tile([P, PACK, HALF], F32, name=f"w_raw{v}") for v in range(2)]
+        w_raw = [keep.tile([P, PACK, HALF], F32, name=f"w_raw{v}") for v in range(N // HALF)]
 
         nc.vector.memset(scale_table[:].bitcast(I32), 0)
         nc.sync.dma_start(offs_sb[:], offs)
-        words_in = x_words[0].rearrange("p n t -> p (n t)").bitcast(I32)
+        words_in = x_words[0].rearrange("p n j -> p (n j)").bitcast(I32)
         nc.sync.dma_start(word_table[:, 0:FIRST_WORDS], words_in[:, 0:FIRST_WORDS])
-        for q in range(4):
+        for q in range(P // QUADRANT):
             nc.sync.dma_start(
-                scale_table[32 * q : 32 * q + 4, :].bitcast(I32),
-                x_scales[0, 4 * q : 4 * q + 4, :].bitcast(I32),
+                scale_table[QUADRANT * q : QUADRANT * q + PACK, :].bitcast(I32),
+                x_scales[0, PACK * q : PACK * (q + 1), :].bitcast(I32),
             )
         nc.sync.dma_start(word_table[:, FIRST_WORDS:T], words_in[:, FIRST_WORDS:T])
         w_rows = w1.rearrange("(p j) c -> p j c", j=PACK)
-        for v in range(2):
+        for v in range(N // HALF):
             nc.sync.dma_start(w_raw[v][:], w_rows[:, :, v * HALF : (v + 1) * HALF])
         nc.sync.dma_start(own_sb[:], own)
+
         res_rows = res.rearrange("(p t) c -> p t c", t=PACK)
         out_rows = out_0.rearrange("(p t) c -> p t c", t=PACK)
         res_sb = []
         for i, (c0, n) in enumerate(PIECES):
-            rows = []
-            group = 2 if i == 0 else PACK
+            slots = []
+            group = PAIR if i == 0 else PACK
             for t0 in range(0, PACK, group):
-                r = keep.tile([P, group, n], F32, name=f"res{i}_{t0}", tag=f"res{i}_{t0}", align_bytes=64)
+                r = keep.tile([P, group, n], F32, name=f"res{i}_{t0}", align_bytes=64)
                 nc.sync.dma_start(r[:], res_rows[:, t0 : t0 + group, c0 : c0 + n])
-                rows.extend([r[:, e, :] for e in range(group)])
-            res_sb.append(rows)
+                slots.extend([r[:, e, :] for e in range(group)])
+            res_sb.append(slots)
 
         x_scale = keep.tile([P, S], U8, name="x_scale", align_bytes=64)
         x_code = keep.tile([P, S], U32, name="x_code", align_bytes=64)
         nc.vector.tensor_copy(x_scale[:], scale_table[:].indirect(offs_sb[:]))
         nc.vector.tensor_copy(x_code[:], word_table[:].bitcast(U32).indirect(offs_sb[:]))
 
-        w_src = [w_raw[v][:].rearrange("p j (m t) -> p m j t", t=PACK) for v in range(2)]
+        w_src = [w_raw[v][:].rearrange("p j (m t) -> p m j t", t=PACK) for v in range(N // HALF)]
         w_bf = keep.tile([P, PACK, P, PACK], BF16, name="w_bf", align_bytes=64)
         w_dst = w_bf[:].rearrange("p t m j -> p m j t")
-        for v, t0, t1 in ((0, 0, 4), (1, 0, 2), (1, 2, 4)):
-            nc.scalar.copy(w_dst[:, v * 64 : (v + 1) * 64, :, t0:t1], w_src[v][:, :, :, t0:t1])
+        m_half = HALF // PACK
+        for v, t0, t1 in WEIGHT_COPIES:
+            nc.scalar.copy(w_dst[:, v * m_half : (v + 1) * m_half, :, t0:t1], w_src[v][:, :, :, t0:t1])
         w_code = []
         w_scale = []
         for t in range(PACK):
-            c = keep.tile([P, P], U32, name=f"w_code{t}", align_bytes=64)
-            sc = keep.tile([P, P], U8, name=f"w_scale{t}", align_bytes=64)
+            codes = keep.tile([P, P], U32, name=f"w_code{t}", align_bytes=64)
+            scales = keep.tile([P, P], U8, name=f"w_scale{t}", align_bytes=64)
             nc.vector.quantize_mx(
-                out=c[:].bitcast(FP8X4),
-                scales=sc[:],
+                out=codes[:].bitcast(FP8X4),
+                scales=scales[:],
                 in_=w_bf[:, t, :, :].rearrange("p m j -> p (m j)"),
             )
-            w_code.append(c)
-            w_scale.append(sc)
+            w_code.append(codes)
+            w_scale.append(scales)
 
         y = []
         for t in range(PACK):
             yt = keep.tile([P, S], F32, name=f"y{t}")
             for h in range(S // BANK):
+                cols = slice(h * BANK, (h + 1) * BANK)
                 acc = psum.tile([P, BANK], F32, name=f"acc{t}_{h}")
                 nc.tensor.matmul_mx(
                     out=acc[:],
                     lhsT=w_code[t][:].bitcast(FP8X4),
                     lhsT_scale=w_scale[t][:],
-                    rhs=x_code[:, h * BANK : (h + 1) * BANK].bitcast(FP8X4),
-                    rhs_scale=x_scale[:, h * BANK : (h + 1) * BANK],
+                    rhs=x_code[:, cols].bitcast(FP8X4),
+                    rhs_scale=x_scale[:, cols],
                     start=True,
                     stop=True,
                 )
                 if (t, h) == (0, 1):
-                    nc.vector.tensor_scalar_max(yt[:, h * BANK : (h + 1) * BANK], acc[:], 0.0)
+                    nc.vector.tensor_scalar_max(yt[:, cols], acc[:], 0.0)
                 else:
-                    nc.scalar.activation(yt[:, h * BANK : (h + 1) * BANK], acc[:], RELU)
+                    nc.scalar.activation(yt[:, cols], acc[:], RELU)
             y.append(yt)
 
+        stretches = U // STRETCH
         o_scale = keep.tile([P, STRETCH], U8, name="o_scale", align_bytes=64)
-        o_code = [keep.tile([P, STRETCH], U32, name=f"o_code{s}", align_bytes=64) for s in range(U // STRETCH)]
-        rounded = [keep.tile([P, n, PACK], BF16, name=f"rounded{c0}", align_bytes=64) for c0, n in RUNS]
-        words_dram = out_1[0].rearrange("p n t -> p (n t)")
+        o_code = [keep.tile([P, STRETCH], U32, name=f"o_code{s}", align_bytes=64) for s in range(stretches)]
+        rounded = [keep.tile([P, m, PACK], BF16, name=f"rounded{r0}", align_bytes=64) for r0, m in RUNS]
+        words_out = out_1[0].rearrange("p n j -> p (n j)")
         for i, (c0, n) in enumerate(PIECES):
-            summed = keep.tile([P, PACK, n], F32, name=f"summed{i}", tag=f"summed{i}", align_bytes=64)
-            group = 2 if n >= STRETCH else PACK
+            summed = keep.tile([P, PACK, n], F32, name=f"summed{i}", align_bytes=64)
             for t in range(PACK):
                 nc.vector.tensor_tensor(
                     summed[:, t, :],
@@ -122,31 +129,36 @@ def tile_picked_unmerge_relu_po_kernel(tc, x_words, x_scales, w1, res, offs, own
                     res_sb[i][t],
                     ADD,
                 )
-                if (t + 1) % group == 0:
-                    rows = slice(t + 1 - group, t + 1)
-                    nc.sync.dma_start(out_rows[:, rows, c0 : c0 + n], summed[:, rows, :])
+                if (t + 1) % PAIR == 0:
+                    pair = slice(t + 1 - PAIR, t + 1)
+                    nc.sync.dma_start(out_rows[:, pair, c0 : c0 + n], summed[:, pair, :])
+
             for (r0, m), run in zip(RUNS, rounded):
                 lo, hi = max(r0, c0), min(r0 + m, c0 + n)
                 if lo >= hi:
                     continue
                 nc.scalar.copy(
-                    run[:, lo - r0 : hi - r0, :].rearrange("p (c i) t -> p c t i", i=4),
-                    summed[:, :, lo - c0 : hi - c0].rearrange("p t (c i) -> p c t i", i=4),
+                    run[:, lo - r0 : hi - r0, :].rearrange("p (c e) t -> p c t e", e=LINE),
+                    summed[:, :, lo - c0 : hi - c0].rearrange("p t (c e) -> p c t e", e=LINE),
                 )
                 if hi == r0 + m:
                     s, o = divmod(r0, STRETCH)
                     nc.vector.quantize_mx(
                         out=o_code[s][:, o : o + m].bitcast(FP8X4),
-                        scales=o_scale[4 * s : P, o : o + m],
+                        scales=o_scale[PACK * s : P, o : o + m],
                         in_=run[:].rearrange("p n t -> p (n t)"),
                     )
-            for z in WORDS_AFTER.get(i, ()):
-                nc.sync.dma_start(
-                    words_dram[:, 4 * z * STRETCH : 4 * (z + 1) * STRETCH].bitcast(I32), o_code[z][:].bitcast(I32)
-                )
-        scales_dram = out_2[0].rearrange("r (s c) -> s r c", c=STRETCH)
-        for q in range(4):
+
+            for s in range(stretches):
+                if min(s + 1, len(PIECES) - 1) == i:
+                    nc.sync.dma_start(
+                        words_out[:, PACK * s * STRETCH : PACK * (s + 1) * STRETCH].bitcast(I32),
+                        o_code[s][:].bitcast(I32),
+                    )
+
+        scales_out = out_2[0].rearrange("r (s c) -> s r c", c=STRETCH)
+        for q in range(P // QUADRANT):
             nc.sync.dma_start(
-                scales_dram[:, 4 * q : 4 * q + 4, :].bitcast(I32),
-                o_scale[32 * q : 32 * q + 16, :].bitcast(I32),
+                scales_out[:, PACK * q : PACK * (q + 1), :].bitcast(I32),
+                o_scale[QUADRANT * q : QUADRANT * q + PACK * stretches, :].bitcast(I32),
             )

@@ -22,40 +22,42 @@ QUADRANT = 32
 BANK = 512
 STRIPE = 16
 LINE = 4
-HALF = N // 2
-FIRST_WORDS = 512
+FIRST_WORDS = 256
 STRETCH = 512
 
 PIECES = [(0, 768), (768, 768), (1536, 384), (1920, 128)]
 RUNS = [(0, 512), (512, 512), (1024, 512), (1536, 256), (1792, 128), (1920, 128)]
-WEIGHT_COPIES = [(0, 0, PACK), (1, 0, PAIR), (1, PAIR, PACK)]
+W_LOADS = [(0, 256), (256, 256)]
+WEIGHT_COPIES = [(0, 0, PACK), (1, 0, 1), (1, 1, PACK)]
+FIRST_PARTS = [(0, 256, True), (256, 256, False), (512, 256, True), (768, 256, False)]
 
 
 def tile_picked_unmerge_relu_po_kernel(tc, x_words, x_scales, w1, res, offs, own, out_0, out_1, out_2):
     nc = tc.nc
     with ExitStack() as ctx:
         keep = ctx.enter_context(tc.tile_pool(name="keep", bufs=1))
-        psum = ctx.enter_context(tc.psum_pool(name="psum", bufs=1))
+        psum = ctx.enter_context(tc.psum_pool(name="psum", bufs=8))
 
         offs_sb = keep.tile([P, S // STRIPE], U16, name="offs_sb")
         own_sb = keep.tile([P, U // STRIPE], U16, name="own_sb")
         scale_table = keep.tile([P, T], U8, name="scale_table", align_bytes=64)
         word_table = keep.tile([P, T], I32, name="word_table", align_bytes=64)
-        w_raw = [keep.tile([P, PACK, HALF], F32, name=f"w_raw{v}") for v in range(N // HALF)]
+        w_raw = [keep.tile([P, PACK, n], F32, name=f"w_raw{c0}") for c0, n in W_LOADS]
 
         nc.vector.memset(scale_table[:].bitcast(I32), 0)
         nc.sync.dma_start(offs_sb[:], offs)
         words_in = x_words[0].rearrange("p n j -> p (n j)").bitcast(I32)
         nc.sync.dma_start(word_table[:, 0:FIRST_WORDS], words_in[:, 0:FIRST_WORDS])
         for q in range(P // QUADRANT):
-            nc.sync.dma_start(
+            queue = nc.sync if q % 2 == 0 else nc.scalar
+            queue.dma_start(
                 scale_table[QUADRANT * q : QUADRANT * q + PACK, :].bitcast(I32),
                 x_scales[0, PACK * q : PACK * (q + 1), :].bitcast(I32),
             )
         nc.sync.dma_start(word_table[:, FIRST_WORDS:T], words_in[:, FIRST_WORDS:T])
         w_rows = w1.rearrange("(p j) c -> p j c", j=PACK)
-        for v in range(N // HALF):
-            nc.sync.dma_start(w_raw[v][:], w_rows[:, :, v * HALF : (v + 1) * HALF])
+        for raw, (c0, n) in zip(w_raw, W_LOADS):
+            nc.sync.dma_start(raw[:], w_rows[:, :, c0 : c0 + n])
         nc.sync.dma_start(own_sb[:], own)
 
         res_rows = res.rearrange("(p t) c -> p t c", t=PACK)
@@ -75,12 +77,12 @@ def tile_picked_unmerge_relu_po_kernel(tc, x_words, x_scales, w1, res, offs, own
         nc.vector.tensor_copy(x_scale[:], scale_table[:].indirect(offs_sb[:]))
         nc.vector.tensor_copy(x_code[:], word_table[:].bitcast(U32).indirect(offs_sb[:]))
 
-        w_src = [w_raw[v][:].rearrange("p j (m t) -> p m j t", t=PACK) for v in range(N // HALF)]
+        w_src = [raw[:].rearrange("p j (m t) -> p m j t", t=PACK) for raw in w_raw]
         w_bf = keep.tile([P, PACK, P, PACK], BF16, name="w_bf", align_bytes=64)
         w_dst = w_bf[:].rearrange("p t m j -> p m j t")
-        m_half = HALF // PACK
         for v, t0, t1 in WEIGHT_COPIES:
-            nc.scalar.copy(w_dst[:, v * m_half : (v + 1) * m_half, :, t0:t1], w_src[v][:, :, :, t0:t1])
+            c0, n = W_LOADS[v]
+            nc.scalar.copy(w_dst[:, c0 // PACK : (c0 + n) // PACK, :, t0:t1], w_src[v][:, :, :, t0:t1])
         w_code = []
         w_scale = []
         for t in range(PACK):
@@ -97,9 +99,10 @@ def tile_picked_unmerge_relu_po_kernel(tc, x_words, x_scales, w1, res, offs, own
         y = []
         for t in range(PACK):
             yt = keep.tile([P, S], F32, name=f"y{t}")
-            for h in range(S // BANK):
-                cols = slice(h * BANK, (h + 1) * BANK)
-                acc = psum.tile([P, BANK], F32, name=f"acc{t}_{h}")
+            parts = FIRST_PARTS if t == 0 else [(0, BANK, False), (BANK, BANK, False)]
+            for c0, n, on_vector in parts:
+                cols = slice(c0, c0 + n)
+                acc = psum.tile([P, n], F32, name="acc")
                 nc.tensor.matmul_mx(
                     out=acc[:],
                     lhsT=w_code[t][:].bitcast(FP8X4),
@@ -109,7 +112,7 @@ def tile_picked_unmerge_relu_po_kernel(tc, x_words, x_scales, w1, res, offs, own
                     start=True,
                     stop=True,
                 )
-                if (t, h) == (0, 1):
+                if on_vector:
                     nc.vector.tensor_scalar_max(yt[:, cols], acc[:], 0.0)
                 else:
                     nc.scalar.activation(yt[:, cols], acc[:], RELU)

@@ -28,8 +28,8 @@ STRETCH = 512
 PIECES = [(0, 768), (768, 768), (1536, 384), (1920, 128)]
 RUNS = [(0, 512), (512, 512), (1024, 512), (1536, 256), (1792, 128), (1920, 128)]
 W_LOADS = [(0, 256), (256, 256)]
-WEIGHT_COPIES = [(0, 0, PACK), (1, 0, 1), (1, 1, PACK)]
-FIRST_PARTS = [(0, 256, True), (256, 256, False), (512, 256, True), (768, 256, False)]
+EARLY = 768
+FIRST_PARTS = [(0, 256, False), (256, 256, False), (512, 256, True), (768, 256, False)]
 
 
 def tile_picked_unmerge_relu_po_kernel(tc, x_words, x_scales, w1, res, offs, own, out_0, out_1, out_2):
@@ -73,28 +73,46 @@ def tile_picked_unmerge_relu_po_kernel(tc, x_words, x_scales, w1, res, offs, own
             res_sb.append(slots)
 
         x_scale = keep.tile([P, S], U8, name="x_scale", align_bytes=64)
-        x_code = keep.tile([P, S], U32, name="x_code", align_bytes=64)
+        early_code = keep.tile([P, EARLY], U32, name="early_code", align_bytes=64)
+        words = word_table[:].bitcast(U32)
         nc.vector.tensor_copy(x_scale[:], scale_table[:].indirect(offs_sb[:]))
-        nc.vector.tensor_copy(x_code[:], word_table[:].bitcast(U32).indirect(offs_sb[:]))
+        nc.vector.tensor_copy(early_code[:], words.indirect(offs_sb[:, 0 : EARLY // STRIPE]))
 
         w_src = [raw[:].rearrange("p j (m t) -> p m j t", t=PACK) for raw in w_raw]
-        w_bf = keep.tile([P, PACK, P, PACK], BF16, name="w_bf", align_bytes=64)
-        w_dst = w_bf[:].rearrange("p t m j -> p m j t")
-        for v, t0, t1 in WEIGHT_COPIES:
-            c0, n = W_LOADS[v]
-            nc.scalar.copy(w_dst[:, c0 // PACK : (c0 + n) // PACK, :, t0:t1], w_src[v][:, :, :, t0:t1])
+        w_first = keep.tile([P, 1, P, PACK], BF16, name="w_first", tag="first", align_bytes=64)
+        w_rest = keep.tile([P, PACK - 1, P, PACK], BF16, name="w_rest", align_bytes=64)
+        for src, (c0, n) in zip(w_src, W_LOADS):
+            ms = slice(c0 // PACK, (c0 + n) // PACK)
+            nc.scalar.copy(w_first[:].rearrange("p t m j -> p m j t")[:, ms, :, :], src[:, :, :, 0:1])
+            nc.scalar.copy(w_rest[:].rearrange("p t m j -> p m j t")[:, ms, :, :], src[:, :, :, 1:PACK])
         w_code = []
         w_scale = []
         for t in range(PACK):
             codes = keep.tile([P, P], U32, name=f"w_code{t}", align_bytes=64)
             scales = keep.tile([P, P], U8, name=f"w_scale{t}", align_bytes=64)
+            w_bf = w_first[:, 0, :, :] if t == 0 else w_rest[:, t - 1, :, :]
             nc.vector.quantize_mx(
                 out=codes[:].bitcast(FP8X4),
                 scales=scales[:],
-                in_=w_bf[:, t, :, :].rearrange("p m j -> p (m j)"),
+                in_=w_bf.rearrange("p m j -> p (m j)"),
             )
             w_code.append(codes)
             w_scale.append(scales)
+            if t == 0:
+                late_code = keep.tile([P, S - EARLY], U32, name="late_code", tag="first", align_bytes=64)
+                nc.vector.tensor_copy(late_code[:], words.indirect(offs_sb[:, EARLY // STRIPE : S // STRIPE]))
+
+        def product(out, t, c0, n):
+            codes = early_code[:, c0 : c0 + n] if c0 < EARLY else late_code[:, c0 - EARLY : c0 - EARLY + n]
+            nc.tensor.matmul_mx(
+                out=out,
+                lhsT=w_code[t][:].bitcast(FP8X4),
+                lhsT_scale=w_scale[t][:],
+                rhs=codes.bitcast(FP8X4),
+                rhs_scale=x_scale[:, c0 : c0 + n],
+                start=True,
+                stop=True,
+            )
 
         y = []
         for t in range(PACK):
@@ -103,15 +121,10 @@ def tile_picked_unmerge_relu_po_kernel(tc, x_words, x_scales, w1, res, offs, own
             for c0, n, on_vector in parts:
                 cols = slice(c0, c0 + n)
                 acc = psum.tile([P, n], F32, name="acc")
-                nc.tensor.matmul_mx(
-                    out=acc[:],
-                    lhsT=w_code[t][:].bitcast(FP8X4),
-                    lhsT_scale=w_scale[t][:],
-                    rhs=x_code[:, cols].bitcast(FP8X4),
-                    rhs_scale=x_scale[:, cols],
-                    start=True,
-                    stop=True,
-                )
+                cut = min(n, EARLY - c0) if c0 < EARLY else n
+                product(acc[:, 0:cut], t, c0, cut)
+                if cut < n:
+                    product(acc[:, cut:n], t, c0 + cut, n - cut)
                 if on_vector:
                     nc.vector.tensor_scalar_max(yt[:, cols], acc[:], 0.0)
                 else:

@@ -25,9 +25,9 @@ LINE = 4
 FIRST_WORDS = 256
 STRETCH = 512
 
-PIECES = [(0, 768), (768, 768), (1536, 384), (1920, 128)]
+PIECES = [(0, 960), (960, 640), (1600, 320), (1920, 128)]
 RUNS = [(0, 512), (512, 512), (1024, 512), (1536, 256), (1792, 128), (1920, 128)]
-W_LOADS = [(0, 256), (256, 256)]
+W_LOADS = [(0, 192), (192, 320)]
 EARLY = 768
 FIRST_PARTS = [(0, 256, False), (256, 256, False), (512, 256, True), (768, 256, False)]
 
@@ -54,10 +54,11 @@ def tile_picked_unmerge_relu_po_kernel(tc, x_words, x_scales, w1, res, offs, own
                 scale_table[QUADRANT * q : QUADRANT * q + PACK, :].bitcast(I32),
                 x_scales[0, PACK * q : PACK * (q + 1), :].bitcast(I32),
             )
-        nc.sync.dma_start(word_table[:, FIRST_WORDS:T], words_in[:, FIRST_WORDS:T])
         w_rows = w1.rearrange("(p j) c -> p j c", j=PACK)
         for raw, (c0, n) in zip(w_raw, W_LOADS):
             nc.sync.dma_start(raw[:], w_rows[:, :, c0 : c0 + n])
+            if c0 == 0:
+                nc.sync.dma_start(word_table[:, FIRST_WORDS:T], words_in[:, FIRST_WORDS:T])
         nc.sync.dma_start(own_sb[:], own)
 
         res_rows = res.rearrange("(p t) c -> p t c", t=PACK)

@@ -20,29 +20,31 @@ PACK = 4
 PAIR = 2
 QUADRANT = 32
 BANK = 512
+BANKS = 8
 STRIPE = 16
 LINE = 4
-FIRST_WORDS = 256
+HALF = N // 2
 STRETCH = 512
+FIRST_WORDS = 384
+EARLY = 768
 
+FIRST_PARTS = [(0, 256, False), (256, 256, False), (512, 256, False), (768, 128, True), (896, 128, False)]
+OTHER_PARTS = [(0, BANK, False), (BANK, BANK, False)]
 PIECES = [(0, 960), (960, 640), (1600, 320), (1920, 128)]
 RUNS = [(0, 512), (512, 512), (1024, 512), (1536, 256), (1792, 128), (1920, 128)]
-W_LOADS = [(0, 192), (192, 320)]
-EARLY = 768
-FIRST_PARTS = [(0, 256, False), (256, 256, False), (512, 256, True), (768, 256, False)]
 
 
 def tile_picked_unmerge_relu_po_kernel(tc, x_words, x_scales, w1, res, offs, own, out_0, out_1, out_2):
     nc = tc.nc
     with ExitStack() as ctx:
         keep = ctx.enter_context(tc.tile_pool(name="keep", bufs=1))
-        psum = ctx.enter_context(tc.psum_pool(name="psum", bufs=8))
+        psum = ctx.enter_context(tc.psum_pool(name="psum", bufs=BANKS))
 
         offs_sb = keep.tile([P, S // STRIPE], U16, name="offs_sb")
         own_sb = keep.tile([P, U // STRIPE], U16, name="own_sb")
         scale_table = keep.tile([P, T], U8, name="scale_table", align_bytes=64)
         word_table = keep.tile([P, T], I32, name="word_table", align_bytes=64)
-        w_raw = [keep.tile([P, PACK, n], F32, name=f"w_raw{c0}") for c0, n in W_LOADS]
+        w_raw = [keep.tile([P, PACK, HALF], F32, name=f"w_raw{v * HALF}") for v in range(N // HALF)]
 
         nc.vector.memset(scale_table[:].bitcast(I32), 0)
         nc.sync.dma_start(offs_sb[:], offs)
@@ -55,10 +57,9 @@ def tile_picked_unmerge_relu_po_kernel(tc, x_words, x_scales, w1, res, offs, own
                 x_scales[0, PACK * q : PACK * (q + 1), :].bitcast(I32),
             )
         w_rows = w1.rearrange("(p j) c -> p j c", j=PACK)
-        for raw, (c0, n) in zip(w_raw, W_LOADS):
-            nc.sync.dma_start(raw[:], w_rows[:, :, c0 : c0 + n])
-            if c0 == 0:
-                nc.sync.dma_start(word_table[:, FIRST_WORDS:T], words_in[:, FIRST_WORDS:T])
+        nc.sync.dma_start(w_raw[0][:], w_rows[:, :, 0:HALF])
+        nc.sync.dma_start(word_table[:, FIRST_WORDS:T], words_in[:, FIRST_WORDS:T])
+        nc.sync.dma_start(w_raw[1][:], w_rows[:, :, HALF:N])
         nc.sync.dma_start(own_sb[:], own)
 
         res_rows = res.rearrange("(p t) c -> p t c", t=PACK)
@@ -82,8 +83,8 @@ def tile_picked_unmerge_relu_po_kernel(tc, x_words, x_scales, w1, res, offs, own
         w_src = [raw[:].rearrange("p j (m t) -> p m j t", t=PACK) for raw in w_raw]
         w_first = keep.tile([P, 1, P, PACK], BF16, name="w_first", tag="first", align_bytes=64)
         w_rest = keep.tile([P, PACK - 1, P, PACK], BF16, name="w_rest", align_bytes=64)
-        for src, (c0, n) in zip(w_src, W_LOADS):
-            ms = slice(c0 // PACK, (c0 + n) // PACK)
+        for v, src in enumerate(w_src):
+            ms = slice(v * HALF // PACK, (v + 1) * HALF // PACK)
             nc.scalar.copy(w_first[:].rearrange("p t m j -> p m j t")[:, ms, :, :], src[:, :, :, 0:1])
             nc.scalar.copy(w_rest[:].rearrange("p t m j -> p m j t")[:, ms, :, :], src[:, :, :, 1:PACK])
         w_code = []
@@ -103,14 +104,14 @@ def tile_picked_unmerge_relu_po_kernel(tc, x_words, x_scales, w1, res, offs, own
                 late_code = keep.tile([P, S - EARLY], U32, name="late_code", tag="first", align_bytes=64)
                 nc.vector.tensor_copy(late_code[:], words.indirect(offs_sb[:, EARLY // STRIPE : S // STRIPE]))
 
-        def product(out, t, c0, n):
-            codes = early_code[:, c0 : c0 + n] if c0 < EARLY else late_code[:, c0 - EARLY : c0 - EARLY + n]
+        def product(out, t, e0, n):
+            x_code = early_code[:, e0 : e0 + n] if e0 < EARLY else late_code[:, e0 - EARLY : e0 - EARLY + n]
             nc.tensor.matmul_mx(
                 out=out,
                 lhsT=w_code[t][:].bitcast(FP8X4),
                 lhsT_scale=w_scale[t][:],
-                rhs=codes.bitcast(FP8X4),
-                rhs_scale=x_scale[:, c0 : c0 + n],
+                rhs=x_code.bitcast(FP8X4),
+                rhs_scale=x_scale[:, e0 : e0 + n],
                 start=True,
                 stop=True,
             )
@@ -118,18 +119,16 @@ def tile_picked_unmerge_relu_po_kernel(tc, x_words, x_scales, w1, res, offs, own
         y = []
         for t in range(PACK):
             yt = keep.tile([P, S], F32, name=f"y{t}")
-            parts = FIRST_PARTS if t == 0 else [(0, BANK, False), (BANK, BANK, False)]
-            for c0, n, on_vector in parts:
-                cols = slice(c0, c0 + n)
+            for e0, n, on_vector in FIRST_PARTS if t == 0 else OTHER_PARTS:
                 acc = psum.tile([P, n], F32, name="acc")
-                cut = min(n, EARLY - c0) if c0 < EARLY else n
-                product(acc[:, 0:cut], t, c0, cut)
+                cut = min(n, EARLY - e0) if e0 < EARLY else n
+                product(acc[:, 0:cut], t, e0, cut)
                 if cut < n:
-                    product(acc[:, cut:n], t, c0 + cut, n - cut)
+                    product(acc[:, cut:n], t, e0 + cut, n - cut)
                 if on_vector:
-                    nc.vector.tensor_scalar_max(yt[:, cols], acc[:], 0.0)
+                    nc.vector.tensor_scalar_max(yt[:, e0 : e0 + n], acc[:], 0.0)
                 else:
-                    nc.scalar.activation(yt[:, cols], acc[:], RELU)
+                    nc.scalar.activation(yt[:, e0 : e0 + n], acc[:], RELU)
             y.append(yt)
 
         stretches = U // STRETCH
@@ -137,8 +136,18 @@ def tile_picked_unmerge_relu_po_kernel(tc, x_words, x_scales, w1, res, offs, own
         o_code = [keep.tile([P, STRETCH], U32, name=f"o_code{s}", align_bytes=64) for s in range(stretches)]
         rounded = [keep.tile([P, m, PACK], BF16, name=f"rounded{r0}", align_bytes=64) for r0, m in RUNS]
         words_out = out_1[0].rearrange("p n j -> p (n j)")
+
+        def store_words(first, cols):
+            s, o = divmod(first, STRETCH)
+            nc.sync.dma_start(
+                words_out[:, PACK * first : PACK * (first + cols)].bitcast(I32),
+                o_code[s][:, o : o + cols].bitcast(I32),
+            )
+
+        last_piece = len(PIECES) - 1
         for i, (c0, n) in enumerate(PIECES):
             summed = keep.tile([P, PACK, n], F32, name=f"summed{i}", align_bytes=64)
+            group = PAIR if i < last_piece else PACK
             for t in range(PACK):
                 nc.vector.tensor_tensor(
                     summed[:, t, :],
@@ -146,9 +155,11 @@ def tile_picked_unmerge_relu_po_kernel(tc, x_words, x_scales, w1, res, offs, own
                     res_sb[i][t],
                     ADD,
                 )
-                if (t + 1) % PAIR == 0:
-                    pair = slice(t + 1 - PAIR, t + 1)
-                    nc.sync.dma_start(out_rows[:, pair, c0 : c0 + n], summed[:, pair, :])
+                if (t + 1) % group == 0:
+                    done = slice(t + 1 - group, t + 1)
+                    nc.sync.dma_start(out_rows[:, done, c0 : c0 + n], summed[:, done, :])
+                if t + 1 == PAIR and 0 < i < last_piece:
+                    store_words((i - 1) * STRETCH, STRETCH)
 
             for (r0, m), run in zip(RUNS, rounded):
                 lo, hi = max(r0, c0), min(r0 + m, c0 + n)
@@ -166,12 +177,10 @@ def tile_picked_unmerge_relu_po_kernel(tc, x_words, x_scales, w1, res, offs, own
                         in_=run[:].rearrange("p n t -> p (n t)"),
                     )
 
-            for s in range(stretches):
-                if min(s + 1, len(PIECES) - 1) == i:
-                    nc.sync.dma_start(
-                        words_out[:, PACK * s * STRETCH : PACK * (s + 1) * STRETCH].bitcast(I32),
-                        o_code[s][:].bitcast(I32),
-                    )
+        last_run, last_cols = RUNS[-1]
+        store_words(U - 2 * STRETCH, STRETCH)
+        store_words(U - STRETCH, STRETCH - last_cols)
+        store_words(last_run, last_cols)
 
         scales_out = out_2[0].rearrange("r (s c) -> s r c", c=STRETCH)
         for q in range(P // QUADRANT):

@@ -23,7 +23,6 @@ BANK = 512
 BANKS = 8
 STRIPE = 16
 LINE = 4
-HALF = N // 2
 STRETCH = 512
 FIRST_WORDS = 384
 EARLY = 768
@@ -44,7 +43,7 @@ def tile_picked_unmerge_relu_po_kernel(tc, x_words, x_scales, w1, res, offs, own
         own_sb = keep.tile([P, U // STRIPE], U16, name="own_sb")
         scale_table = keep.tile([P, T], U8, name="scale_table", align_bytes=64)
         word_table = keep.tile([P, T], I32, name="word_table", align_bytes=64)
-        w_raw = [keep.tile([P, PACK, HALF], F32, name=f"w_raw{v * HALF}") for v in range(N // HALF)]
+        w_raw = [keep.tile([P, PAIR, N], F32, name=f"w_raw{j0}") for j0 in range(0, PACK, PAIR)]
 
         nc.vector.memset(scale_table[:].bitcast(I32), 0)
         nc.sync.dma_start(offs_sb[:], offs)
@@ -57,9 +56,9 @@ def tile_picked_unmerge_relu_po_kernel(tc, x_words, x_scales, w1, res, offs, own
                 x_scales[0, PACK * q : PACK * (q + 1), :].bitcast(I32),
             )
         w_rows = w1.rearrange("(p j) c -> p j c", j=PACK)
-        nc.sync.dma_start(w_raw[0][:], w_rows[:, :, 0:HALF])
+        nc.sync.dma_start(w_raw[0][:], w_rows[:, 0:PAIR, :])
         nc.sync.dma_start(word_table[:, FIRST_WORDS:T], words_in[:, FIRST_WORDS:T])
-        nc.sync.dma_start(w_raw[1][:], w_rows[:, :, HALF:N])
+        nc.sync.dma_start(w_raw[1][:], w_rows[:, PAIR:PACK, :])
         nc.sync.dma_start(own_sb[:], own)
 
         res_rows = res.rearrange("(p t) c -> p t c", t=PACK)
@@ -84,9 +83,9 @@ def tile_picked_unmerge_relu_po_kernel(tc, x_words, x_scales, w1, res, offs, own
         w_first = keep.tile([P, 1, P, PACK], BF16, name="w_first", tag="first", align_bytes=64)
         w_rest = keep.tile([P, PACK - 1, P, PACK], BF16, name="w_rest", align_bytes=64)
         for v, src in enumerate(w_src):
-            ms = slice(v * HALF // PACK, (v + 1) * HALF // PACK)
-            nc.scalar.copy(w_first[:].rearrange("p t m j -> p m j t")[:, ms, :, :], src[:, :, :, 0:1])
-            nc.scalar.copy(w_rest[:].rearrange("p t m j -> p m j t")[:, ms, :, :], src[:, :, :, 1:PACK])
+            js = slice(v * PAIR, (v + 1) * PAIR)
+            nc.scalar.copy(w_first[:].rearrange("p t m j -> p m j t")[:, :, js, :], src[:, :, :, 0:1])
+            nc.scalar.copy(w_rest[:].rearrange("p t m j -> p m j t")[:, :, js, :], src[:, :, :, 1:PACK])
         w_code = []
         w_scale = []
         for t in range(PACK):

@@ -49,12 +49,10 @@ def tile_picked_unmerge_relu_po_kernel(tc, x_words, x_scales, w1, res, offs, own
         nc.sync.dma_start(offs_sb[:], offs)
         words_in = x_words[0].rearrange("p n j -> p (n j)").bitcast(I32)
         nc.sync.dma_start(word_table[:, 0:FIRST_WORDS], words_in[:, 0:FIRST_WORDS])
-        for q in range(P // QUADRANT):
-            queue = nc.sync if q % 2 == 0 else nc.scalar
-            queue.dma_start(
-                scale_table[QUADRANT * q : QUADRANT * q + PACK, :].bitcast(I32),
-                x_scales[0, PACK * q : PACK * (q + 1), :].bitcast(I32),
-            )
+        scale_rows = x_scales[0].rearrange("(q r) c -> r q c", r=PACK)
+        for r in range(PACK):
+            queue = nc.sync if r % 2 == 0 else nc.scalar
+            queue.dma_start(scale_table[r:P:QUADRANT, :].bitcast(I32), scale_rows[r].bitcast(I32))
         w_rows = w1.rearrange("(p j) c -> p j c", j=PACK)
         nc.sync.dma_start(w_raw[0][:], w_rows[:, 0:PAIR, :])
         nc.sync.dma_start(word_table[:, FIRST_WORDS:T], words_in[:, FIRST_WORDS:T])

@@ -131,7 +131,7 @@ def tile_picked_unmerge_relu_po_kernel(tc, x_words, x_scales, w1, res, offs, own
         stretches = U // STRETCH
         o_scale = keep.tile([P, STRETCH], U8, name="o_scale", align_bytes=64)
         o_code = [keep.tile([P, STRETCH], U32, name=f"o_code{s}", align_bytes=64) for s in range(stretches)]
-        rounded = [keep.tile([P, m, PACK], BF16, name=f"rounded{r0}", align_bytes=64) for r0, m in RUNS]
+        rounded = [keep.tile([P, m, PACK], BF16, name=f"rounded{r0}", align_bytes=64) for r0, m in RUNS[:-1]]
         words_out = out_1[0].rearrange("p n j -> p (n j)")
 
         def store_words(first, cols):
@@ -143,7 +143,9 @@ def tile_picked_unmerge_relu_po_kernel(tc, x_words, x_scales, w1, res, offs, own
 
         last_piece = len(PIECES) - 1
         for i, (c0, n) in enumerate(PIECES):
-            summed = keep.tile([P, PACK, n], F32, name=f"summed{i}", align_bytes=64)
+            summed = keep.tile([P, PACK, n], F32, name=f"summed{i}", tag=f"summed{i}", align_bytes=64)
+            if i == last_piece:
+                rounded.append(keep.tile([P, n, PACK], BF16, name="rounded_last", tag="summed1", align_bytes=64))
             group = PAIR if i < last_piece else PACK
             for t in range(PACK):
                 nc.vector.tensor_tensor(
@@ -177,11 +179,12 @@ def tile_picked_unmerge_relu_po_kernel(tc, x_words, x_scales, w1, res, offs, own
         last_run, last_cols = RUNS[-1]
         store_words(U - 2 * STRETCH, STRETCH)
         store_words(U - STRETCH, STRETCH - last_cols)
-        store_words(last_run, last_cols)
 
         scales_out = out_2[0].rearrange("r (s c) -> s r c", c=STRETCH)
         for q in range(P // QUADRANT):
-            nc.sync.dma_start(
+            queue = nc.sync if q % 2 == 0 else nc.scalar
+            queue.dma_start(
                 scales_out[:, PACK * q : PACK * (q + 1), :].bitcast(I32),
                 o_scale[QUADRANT * q : QUADRANT * q + PACK * stretches, :].bitcast(I32),
             )
+        store_words(last_run, last_cols)

@@ -56,7 +56,8 @@ def tile_picked_unmerge_relu_po_kernel(tc, x_words, x_scales, w1, res, offs, own
         w_rows = w1.rearrange("(p j) c -> p j c", j=PACK)
         nc.sync.dma_start(w_raw[0][:], w_rows[:, 0:PAIR, :])
         nc.sync.dma_start(word_table[:, FIRST_WORDS:T], words_in[:, FIRST_WORDS:T])
-        nc.sync.dma_start(w_raw[1][:], w_rows[:, PAIR:PACK, :])
+        for e in range(PAIR):
+            nc.sync.dma_start(w_raw[1][:, e, :], w_rows[:, PAIR + e, :])
         nc.sync.dma_start(own_sb[:], own)
 
         res_rows = res.rearrange("(p t) c -> p t c", t=PACK)
@@ -82,7 +83,12 @@ def tile_picked_unmerge_relu_po_kernel(tc, x_words, x_scales, w1, res, offs, own
         w_rest = keep.tile([P, PACK - 1, P, PACK], BF16, name="w_rest", align_bytes=64)
         for v, src in enumerate(w_src):
             js = slice(v * PAIR, (v + 1) * PAIR)
-            nc.scalar.copy(w_first[:].rearrange("p t m j -> p m j t")[:, :, js, :], src[:, :, :, 0:1])
+            rows = PAIR if v == 0 else 1
+            for e in range(0, PAIR, rows):
+                nc.scalar.copy(
+                    w_first[:].rearrange("p t m j -> p m j t")[:, :, v * PAIR + e : v * PAIR + e + rows, :],
+                    src[:, :, e : e + rows, 0:1],
+                )
             nc.scalar.copy(w_rest[:].rearrange("p t m j -> p m j t")[:, :, js, :], src[:, :, :, 1:PACK])
         w_code = []
         w_scale = []

@@ -14,6 +14,7 @@ U8 = mybir.dt.uint8
 FP8X4 = mybir.dt.float8_e4m3fn_x4
 ADD = mybir.AluOpType.add
 RELU = mybir.ActivationFunctionType.Relu
+COPY = mybir.ActivationFunctionType.Copy
 
 P = 128
 PACK = 4
@@ -147,6 +148,12 @@ def tile_picked_unmerge_relu_po_kernel(tc, x_words, x_scales, w1, res, offs, own
                 o_code[s][:, o : o + cols].bitcast(I32),
             )
 
+        fetched = []
+        for i, (c0, n) in enumerate(PIECES):
+            g = keep.tile([P, n], F32, name=f"fetched{i}", align_bytes=64)
+            nc.scalar.activation(g[:], y[PACK - 1][:].indirect(own_sb[:, c0 // STRIPE : (c0 + n) // STRIPE]), COPY)
+            fetched.append(g)
+
         last_piece = len(PIECES) - 1
         for i, (c0, n) in enumerate(PIECES):
             summed = keep.tile([P, PACK, n], F32, name=f"summed{i}", tag=f"summed{i}", align_bytes=64)
@@ -156,7 +163,7 @@ def tile_picked_unmerge_relu_po_kernel(tc, x_words, x_scales, w1, res, offs, own
             for t in range(PACK):
                 nc.vector.tensor_tensor(
                     summed[:, t, :],
-                    y[t][:].indirect(own_sb[:, c0 // STRIPE : (c0 + n) // STRIPE]),
+                    y[t][:].indirect(own_sb[:, c0 // STRIPE : (c0 + n) // STRIPE]) if t < PACK - 1 else fetched[i][:],
                     res_sb[i][t],
                     ADD,
                 )

@@ -30,7 +30,7 @@ EARLY = 768
 
 FIRST_PARTS = [(0, 256, False), (256, 256, False), (512, 256, False), (768, 128, True), (896, 128, False)]
 OTHER_PARTS = [(0, BANK, False), (BANK, BANK, False)]
-PIECES = [(0, 960), (960, 640), (1600, 320), (1920, 128)]
+PIECES = [(0, 960, 3), (960, 640, 3), (1600, 320, 2), (1920, 128, 3)]
 RUNS = [(0, 512), (512, 512), (1024, 512), (1536, 256), (1792, 128), (1920, 128)]
 
 
@@ -64,7 +64,7 @@ def tile_picked_unmerge_relu_po_kernel(tc, x_words, x_scales, w1, res, offs, own
         res_rows = res.rearrange("(p t) c -> p t c", t=PACK)
         out_rows = out_0.rearrange("(p t) c -> p t c", t=PACK)
         res_sb = []
-        for i, (c0, n) in enumerate(PIECES):
+        for i, (c0, n, first_slot) in enumerate(PIECES):
             slots = []
             group = PAIR if i == 0 else PACK
             for t0 in range(0, PACK, group):
@@ -148,14 +148,15 @@ def tile_picked_unmerge_relu_po_kernel(tc, x_words, x_scales, w1, res, offs, own
                 o_code[s][:, o : o + cols].bitcast(I32),
             )
 
-        fetched = []
-        for i, (c0, n) in enumerate(PIECES):
-            g = keep.tile([P, n], F32, name=f"fetched{i}", align_bytes=64)
-            nc.scalar.activation(g[:], y[PACK - 1][:].indirect(own_sb[:, c0 // STRIPE : (c0 + n) // STRIPE]), COPY)
-            fetched.append(g)
+        fetched = {}
+        for i, (c0, n, first_slot) in enumerate(PIECES):
+            for t in range(first_slot, PACK):
+                g = keep.tile([P, n], F32, name=f"fetched{i}_{t}", align_bytes=64)
+                nc.scalar.activation(g[:], y[t][:].indirect(own_sb[:, c0 // STRIPE : (c0 + n) // STRIPE]), COPY)
+                fetched[i, t] = g
 
         last_piece = len(PIECES) - 1
-        for i, (c0, n) in enumerate(PIECES):
+        for i, (c0, n, first_slot) in enumerate(PIECES):
             summed = keep.tile([P, PACK, n], F32, name=f"summed{i}", tag=f"summed{i}", align_bytes=64)
             if i == last_piece:
                 rounded.append(keep.tile([P, n, PACK], BF16, name="rounded_last", tag="summed1", align_bytes=64))
@@ -163,7 +164,7 @@ def tile_picked_unmerge_relu_po_kernel(tc, x_words, x_scales, w1, res, offs, own
             for t in range(PACK):
                 nc.vector.tensor_tensor(
                     summed[:, t, :],
-                    y[t][:].indirect(own_sb[:, c0 // STRIPE : (c0 + n) // STRIPE]) if t < PACK - 1 else fetched[i][:],
+                    y[t][:].indirect(own_sb[:, c0 // STRIPE : (c0 + n) // STRIPE]) if t < first_slot else fetched[i, t][:],
                     res_sb[i][t],
                     ADD,
                 )

@@ -30,7 +30,8 @@ EARLY = 768
 
 FIRST_PARTS = [(0, 256, False), (256, 256, False), (512, 256, False), (768, 128, True), (896, 128, False)]
 OTHER_PARTS = [(0, BANK, False), (BANK, BANK, False)]
-PIECES = [(0, 960, 3), (960, 640, 3), (1600, 320, 2), (1920, 128, 3)]
+PIECES = [(0, 960, 3), (960, 640, 3), (1600, 320, 2), (1920, 128, 2)]
+QUANTISED_AFTER = [[0], [], [1], [2, 3, 4, 5]]
 RUNS = [(0, 512), (512, 512), (1024, 512), (1536, 256), (1792, 128), (1920, 128)]
 
 
@@ -137,8 +138,8 @@ def tile_picked_unmerge_relu_po_kernel(tc, x_words, x_scales, w1, res, offs, own
 
         stretches = U // STRETCH
         o_scale = keep.tile([P, STRETCH], U8, name="o_scale", align_bytes=64)
-        o_code = [keep.tile([P, STRETCH], U32, name=f"o_code{s}", align_bytes=64) for s in range(stretches)]
-        rounded = [keep.tile([P, m, PACK], BF16, name=f"rounded{r0}", align_bytes=64) for r0, m in RUNS[:-1]]
+        o_code = {}
+        rounded = [keep.tile([P, m, PACK], BF16, name=f"rounded{r0}", tag=f"rounded{r0}", align_bytes=64) for r0, m in RUNS[:-1]]
         words_out = out_1[0].rearrange("p n j -> p (n j)")
 
         def store_words(first, cols):
@@ -154,6 +155,17 @@ def tile_picked_unmerge_relu_po_kernel(tc, x_words, x_scales, w1, res, offs, own
                 g = keep.tile([P, n], F32, name=f"fetched{i}_{t}", align_bytes=64)
                 nc.scalar.activation(g[:], y[t][:].indirect(own_sb[:, c0 // STRIPE : (c0 + n) // STRIPE]), COPY)
                 fetched[i, t] = g
+
+        def quantise(r):
+            r0, m = RUNS[r]
+            s, o = divmod(r0, STRETCH)
+            if o == 0:
+                o_code[s] = keep.tile([P, STRETCH], U32, name=f"o_code{s}", align_bytes=64)
+            nc.vector.quantize_mx(
+                out=o_code[s][:, o : o + m].bitcast(FP8X4),
+                scales=o_scale[PACK * s : P, o : o + m],
+                in_=rounded[r][:].rearrange("p n t -> p (n t)"),
+            )
 
         last_piece = len(PIECES) - 1
         for i, (c0, n, first_slot) in enumerate(PIECES):
@@ -171,24 +183,20 @@ def tile_picked_unmerge_relu_po_kernel(tc, x_words, x_scales, w1, res, offs, own
                 if (t + 1) % group == 0:
                     done = slice(t + 1 - group, t + 1)
                     nc.sync.dma_start(out_rows[:, done, c0 : c0 + n], summed[:, done, :])
-                if t + 1 == PAIR and 0 < i < last_piece:
-                    store_words((i - 1) * STRETCH, STRETCH)
+                if t + 1 == PAIR and i == 1:
+                    store_words(0, STRETCH)
 
             for (r0, m), run in zip(RUNS, rounded):
                 lo, hi = max(r0, c0), min(r0 + m, c0 + n)
-                if lo >= hi:
-                    continue
-                nc.scalar.copy(
-                    run[:, lo - r0 : hi - r0, :].rearrange("p (c e) t -> p c t e", e=LINE),
-                    summed[:, :, lo - c0 : hi - c0].rearrange("p t (c e) -> p c t e", e=LINE),
-                )
-                if hi == r0 + m:
-                    s, o = divmod(r0, STRETCH)
-                    nc.vector.quantize_mx(
-                        out=o_code[s][:, o : o + m].bitcast(FP8X4),
-                        scales=o_scale[PACK * s : P, o : o + m],
-                        in_=run[:].rearrange("p n t -> p (n t)"),
+                if lo < hi:
+                    nc.scalar.copy(
+                        run[:, lo - r0 : hi - r0, :].rearrange("p (c e) t -> p c t e", e=LINE),
+                        summed[:, :, lo - c0 : hi - c0].rearrange("p t (c e) -> p c t e", e=LINE),
                     )
+            for r in QUANTISED_AFTER[i]:
+                quantise(r)
+            if i == 2:
+                store_words(STRETCH, STRETCH)
 
         last_run, last_cols = RUNS[-1]
         store_words(U - 2 * STRETCH, STRETCH)

@@ -30,7 +30,7 @@ EARLY = 768
 
 FIRST_PARTS = [(0, 256, False), (256, 256, False), (512, 256, False), (768, 128, True), (896, 128, False)]
 OTHER_PARTS = [(0, BANK, False), (BANK, BANK, False)]
-PIECES = [(0, 960, 3), (960, 640, 3), (1600, 320, 2), (1920, 128, 2)]
+PIECES = [(0, 960, 3), (960, 576, 3), (1536, 384, 2), (1920, 128, 2)]
 QUANTISED_AFTER = [[0], [], [1], [2, 3, 4, 5]]
 RUNS = [(0, 512), (512, 512), (1024, 512), (1536, 256), (1792, 128), (1920, 128)]
 

@@ -30,8 +30,8 @@ EARLY = 768
 
 FIRST_PARTS = [(0, 256, False), (256, 256, False), (512, 256, False), (768, 128, True), (896, 128, False)]
 OTHER_PARTS = [(0, BANK, False), (BANK, BANK, False)]
-PIECES = [(0, 960, 3), (960, 576, 3), (1536, 384, 2), (1920, 128, 2)]
-QUANTISED_AFTER = [[0], [], [1], [2, 3, 4, 5]]
+PIECES = [(0, 960, 960), (960, 640, 640), (1600, 448, 896)]
+LAST = 128
 RUNS = [(0, 512), (512, 512), (1024, 512), (1536, 256), (1792, 128), (1920, 128)]
 
 
@@ -65,14 +65,18 @@ def tile_picked_unmerge_relu_po_kernel(tc, x_words, x_scales, w1, res, offs, own
         res_rows = res.rearrange("(p t) c -> p t c", t=PACK)
         out_rows = out_0.rearrange("(p t) c -> p t c", t=PACK)
         res_sb = []
-        for i, (c0, n, first_slot) in enumerate(PIECES):
-            slots = []
+        for i, (c0, n, share) in enumerate(PIECES):
             group = PAIR if i == 0 else PACK
+            parts = []
             for t0 in range(0, PACK, group):
                 r = keep.tile([P, group, n], F32, name=f"res{i}_{t0}", align_bytes=64)
                 nc.sync.dma_start(r[:], res_rows[:, t0 : t0 + group, c0 : c0 + n])
-                slots.extend([r[:, e, :] for e in range(group)])
-            res_sb.append(slots)
+                parts.append(r[:].rearrange("p t c -> p (t c)"))
+            res_sb.append((group * n, parts))
+
+        def res_run(i, lo, hi):
+            size, parts = res_sb[i]
+            return parts[lo // size][:, lo % size : lo % size + hi - lo]
 
         x_scale = keep.tile([P, S], U8, name="x_scale", align_bytes=64)
         early_code = keep.tile([P, EARLY], U32, name="early_code", align_bytes=64)
@@ -149,12 +153,18 @@ def tile_picked_unmerge_relu_po_kernel(tc, x_words, x_scales, w1, res, offs, own
                 o_code[s][:, o : o + cols].bitcast(I32),
             )
 
-        fetched = {}
-        for i, (c0, n, first_slot) in enumerate(PIECES):
-            for t in range(first_slot, PACK):
-                g = keep.tile([P, n], F32, name=f"fetched{i}_{t}", align_bytes=64)
-                nc.scalar.activation(g[:], y[t][:].indirect(own_sb[:, c0 // STRIPE : (c0 + n) // STRIPE]), COPY)
-                fetched[i, t] = g
+        def looked_up(i, t, lo, hi):
+            c0 = PIECES[i][0]
+            return y[t][:].indirect(own_sb[:, (c0 + lo) // STRIPE : (c0 + hi) // STRIPE])
+
+        fetched = []
+        for i, (c0, n, share) in enumerate(PIECES):
+            g = keep.tile([P, share], F32, name=f"fetched{i}", align_bytes=64)
+            first = PACK * n - share
+            for t in range(first // n, PACK):
+                lo = max(first - t * n, 0)
+                nc.scalar.activation(g[:, t * n + lo - first : (t + 1) * n - first], looked_up(i, t, lo, n), COPY)
+            fetched.append(g)
 
         def quantise(r):
             r0, m = RUNS[r]
@@ -167,36 +177,68 @@ def tile_picked_unmerge_relu_po_kernel(tc, x_words, x_scales, w1, res, offs, own
                 in_=rounded[r][:].rearrange("p n t -> p (n t)"),
             )
 
-        last_piece = len(PIECES) - 1
-        for i, (c0, n, first_slot) in enumerate(PIECES):
-            summed = keep.tile([P, PACK, n], F32, name=f"summed{i}", tag=f"summed{i}", align_bytes=64)
-            if i == last_piece:
-                rounded.append(keep.tile([P, n, PACK], BF16, name="rounded_last", tag="summed1", align_bytes=64))
-            group = PAIR if i < last_piece else PACK
-            for t in range(PACK):
-                nc.vector.tensor_tensor(
-                    summed[:, t, :],
-                    y[t][:].indirect(own_sb[:, c0 // STRIPE : (c0 + n) // STRIPE]) if t < first_slot else fetched[i, t][:],
-                    res_sb[i][t],
-                    ADD,
-                )
-                if (t + 1) % group == 0:
-                    done = slice(t + 1 - group, t + 1)
-                    nc.sync.dma_start(out_rows[:, done, c0 : c0 + n], summed[:, done, :])
-                if t + 1 == PAIR and i == 1:
-                    store_words(0, STRETCH)
+        def gather_add(i, t, lo, hi):
+            n = PIECES[i][1]
+            nc.vector.tensor_tensor(
+                summed[i][:, t, lo:hi], looked_up(i, t, lo, hi), res_run(i, t * n + lo, t * n + hi), ADD
+            )
 
+        def add_fetched(i):
+            c0, n, share = PIECES[i]
+            first = PACK * n - share
+            flat = summed[i][:].rearrange("p t c -> p (t c)")
+            nc.vector.tensor_tensor(flat[:, first:], fetched[i][:], res_run(i, first, PACK * n), ADD)
+
+        def store_sums(i, t0, t1, lo, hi):
+            c0 = PIECES[i][0]
+            nc.sync.dma_start(out_rows[:, t0:t1, c0 + lo : c0 + hi], summed[i][:, t0:t1, lo:hi])
+
+        def round_columns(i, first, end):
+            c0 = PIECES[i][0]
             for (r0, m), run in zip(RUNS, rounded):
-                lo, hi = max(r0, c0), min(r0 + m, c0 + n)
+                lo, hi = max(r0, first), min(r0 + m, end)
                 if lo < hi:
                     nc.scalar.copy(
                         run[:, lo - r0 : hi - r0, :].rearrange("p (c e) t -> p c t e", e=LINE),
-                        summed[:, :, lo - c0 : hi - c0].rearrange("p t (c e) -> p c t e", e=LINE),
+                        summed[i][:, :, lo - c0 : hi - c0].rearrange("p t (c e) -> p c t e", e=LINE),
                     )
-            for r in QUANTISED_AFTER[i]:
-                quantise(r)
-            if i == 2:
-                store_words(STRETCH, STRETCH)
+
+        summed = [
+            keep.tile([P, PACK, n], F32, name=f"summed{i}", tag=f"summed{i}", align_bytes=64)
+            for i, (c0, n, share) in enumerate(PIECES)
+        ]
+        for i, (c0, n, share) in enumerate(PIECES[:-1]):
+            first = PACK * n - share
+            for t in range(first // n + 1):
+                hi = min(first - t * n, n)
+                if hi > 0:
+                    gather_add(i, t, 0, hi)
+                if t + 1 == PAIR:
+                    store_sums(i, 0, PAIR, 0, n)
+            add_fetched(i)
+            store_sums(i, PAIR, PACK, 0, n)
+            round_columns(i, c0, c0 + n)
+        quantise(0)
+        store_words(0, STRETCH)
+
+        i = len(PIECES) - 1
+        c0, n, share = PIECES[i]
+        cut = n - LAST
+        add_fetched(i)
+        store_sums(i, PAIR, PACK, 0, n)
+        for t in range(PAIR):
+            gather_add(i, t, 0, cut)
+            store_sums(i, t, t + 1, 0, cut)
+        round_columns(i, c0, c0 + cut)
+        quantise(1)
+        store_words(STRETCH, STRETCH)
+        for t in range(PAIR):
+            gather_add(i, t, cut, n)
+        store_sums(i, 0, PAIR, cut, n)
+        rounded.append(keep.tile([P, LAST, PACK], BF16, name="rounded_last", tag="summed1", align_bytes=64))
+        round_columns(i, c0 + cut, c0 + n)
+        for r in range(2, len(RUNS)):
+            quantise(r)
 
         last_run, last_cols = RUNS[-1]
         store_words(U - 2 * STRETCH, STRETCH)

@@ -30,9 +30,9 @@ EARLY = 768
 
 FIRST_PARTS = [(0, 256, False), (256, 256, False), (512, 256, False), (768, 128, True), (896, 128, False)]
 OTHER_PARTS = [(0, BANK, False), (BANK, BANK, False)]
-PIECES = [(0, 960, 960), (960, 640, 640), (1600, 448, 896)]
-LAST = 128
-RUNS = [(0, 512), (512, 512), (1024, 512), (1536, 256), (1792, 128), (1920, 128)]
+PIECES = [(0, 768), (768, 768), (1536, 512)]
+RUN = 256
+SPLIT = 1280
 
 
 def tile_picked_unmerge_relu_po_kernel(tc, x_words, x_scales, w1, res, offs, own, out_0, out_1, out_2):
@@ -64,19 +64,18 @@ def tile_picked_unmerge_relu_po_kernel(tc, x_words, x_scales, w1, res, offs, own
 
         res_rows = res.rearrange("(p t) c -> p t c", t=PACK)
         out_rows = out_0.rearrange("(p t) c -> p t c", t=PACK)
-        res_sb = []
-        for i, (c0, n, share) in enumerate(PIECES):
-            group = PAIR if i == 0 else PACK
-            parts = []
-            for t0 in range(0, PACK, group):
-                r = keep.tile([P, group, n], F32, name=f"res{i}_{t0}", align_bytes=64)
-                nc.sync.dma_start(r[:], res_rows[:, t0 : t0 + group, c0 : c0 + n])
-                parts.append(r[:].rearrange("p t c -> p (t c)"))
-            res_sb.append((group * n, parts))
+        first_cols = PIECES[0][1]
+        res_sb = {}
+        for t0 in range(0, PACK, PAIR):
+            for c0, n in ((0, first_cols), (first_cols, U - first_cols)):
+                r = keep.tile([P, PAIR, n], F32, name=f"res{t0}_{c0}", align_bytes=64)
+                nc.sync.dma_start(r[:], res_rows[:, t0 : t0 + PAIR, c0 : c0 + n])
+                res_sb[t0, c0] = r
 
-        def res_run(i, lo, hi):
-            size, parts = res_sb[i]
-            return parts[lo // size][:, lo % size : lo % size + hi - lo]
+        def res_piece(i, t0):
+            c0, n = PIECES[i]
+            start = min(c0, first_cols)
+            return res_sb[t0, start][:, :, c0 - start : c0 - start + n]
 
         x_scale = keep.tile([P, S], U8, name="x_scale", align_bytes=64)
         early_code = keep.tile([P, EARLY], U32, name="early_code", align_bytes=64)
@@ -140,109 +139,81 @@ def tile_picked_unmerge_relu_po_kernel(tc, x_words, x_scales, w1, res, offs, own
                     nc.scalar.activation(yt[:, e0 : e0 + n], acc[:], RELU)
             y.append(yt)
 
-        stretches = U // STRETCH
-        o_scale = keep.tile([P, STRETCH], U8, name="o_scale", align_bytes=64)
-        o_code = {}
-        rounded = [keep.tile([P, m, PACK], BF16, name=f"rounded{r0}", tag=f"rounded{r0}", align_bytes=64) for r0, m in RUNS[:-1]]
-        words_out = out_1[0].rearrange("p n j -> p (n j)")
+        def looked_up(i, t):
+            c0, n = PIECES[i]
+            return y[t][:].indirect(own_sb[:, c0 // STRIPE : (c0 + n) // STRIPE])
 
-        def store_words(first, cols):
-            s, o = divmod(first, STRETCH)
-            nc.sync.dma_start(
-                words_out[:, PACK * first : PACK * (first + cols)].bitcast(I32),
-                o_code[s][:, o : o + cols].bitcast(I32),
-            )
+        summed = [keep.tile([P, PACK, n], F32, name=f"summed{c0}", tag=f"summed{c0}", align_bytes=64) for c0, n in PIECES]
+        fetched = [keep.tile([P, PAIR, n], F32, name=f"fetched{c0}", align_bytes=64) for c0, n in PIECES]
+        for i in range(len(PIECES)):
+            for e in range(PAIR):
+                nc.scalar.activation(fetched[i][:, e, :], looked_up(i, PAIR + e), COPY)
 
-        def looked_up(i, t, lo, hi):
-            c0 = PIECES[i][0]
-            return y[t][:].indirect(own_sb[:, (c0 + lo) // STRIPE : (c0 + hi) // STRIPE])
+        def store_sums(i, t0):
+            c0, n = PIECES[i]
+            nc.sync.dma_start(out_rows[:, t0 : t0 + PAIR, c0 : c0 + n], summed[i][:, t0 : t0 + PAIR, :])
 
-        fetched = []
-        for i, (c0, n, share) in enumerate(PIECES):
-            g = keep.tile([P, share], F32, name=f"fetched{i}", align_bytes=64)
-            first = PACK * n - share
-            for t in range(first // n, PACK):
-                lo = max(first - t * n, 0)
-                nc.scalar.activation(g[:, t * n + lo - first : (t + 1) * n - first], looked_up(i, t, lo, n), COPY)
-            fetched.append(g)
-
-        def quantise(r):
-            r0, m = RUNS[r]
-            s, o = divmod(r0, STRETCH)
-            if o == 0:
-                o_code[s] = keep.tile([P, STRETCH], U32, name=f"o_code{s}", align_bytes=64)
-            nc.vector.quantize_mx(
-                out=o_code[s][:, o : o + m].bitcast(FP8X4),
-                scales=o_scale[PACK * s : P, o : o + m],
-                in_=rounded[r][:].rearrange("p n t -> p (n t)"),
-            )
-
-        def gather_add(i, t, lo, hi):
-            n = PIECES[i][1]
-            nc.vector.tensor_tensor(
-                summed[i][:, t, lo:hi], looked_up(i, t, lo, hi), res_run(i, t * n + lo, t * n + hi), ADD
-            )
+        def gather_add(i):
+            for t in range(PAIR):
+                nc.vector.tensor_tensor(summed[i][:, t, :], looked_up(i, t), res_piece(i, 0)[:, t, :], ADD)
+            store_sums(i, 0)
 
         def add_fetched(i):
-            c0, n, share = PIECES[i]
-            first = PACK * n - share
-            flat = summed[i][:].rearrange("p t c -> p (t c)")
-            nc.vector.tensor_tensor(flat[:, first:], fetched[i][:], res_run(i, first, PACK * n), ADD)
+            nc.vector.tensor_tensor(summed[i][:, PAIR:PACK, :], fetched[i][:], res_piece(i, PAIR), ADD)
+            store_sums(i, PAIR)
 
-        def store_sums(i, t0, t1, lo, hi):
-            c0 = PIECES[i][0]
-            nc.sync.dma_start(out_rows[:, t0:t1, c0 + lo : c0 + hi], summed[i][:, t0:t1, lo:hi])
+        gather_add(0)
+        for i in range(1, len(PIECES)):
+            gather_add(i)
+            add_fetched(i - 1)
+        add_fetched(len(PIECES) - 1)
 
-        def round_columns(i, first, end):
-            c0 = PIECES[i][0]
-            for (r0, m), run in zip(RUNS, rounded):
-                lo, hi = max(r0, first), min(r0 + m, end)
-                if lo < hi:
-                    nc.scalar.copy(
-                        run[:, lo - r0 : hi - r0, :].rearrange("p (c e) t -> p c t e", e=LINE),
-                        summed[i][:, :, lo - c0 : hi - c0].rearrange("p t (c e) -> p c t e", e=LINE),
-                    )
+        stretches = U // STRETCH
+        o_scale = keep.tile([P, STRETCH], U8, name="o_scale", align_bytes=64)
+        words_out = out_1[0].rearrange("p n j -> p (n j)")
+        rounded = {}
+        o_code = {}
 
-        summed = [
-            keep.tile([P, PACK, n], F32, name=f"summed{i}", tag=f"summed{i}", align_bytes=64)
-            for i, (c0, n, share) in enumerate(PIECES)
-        ]
-        for i, (c0, n, share) in enumerate(PIECES[:-1]):
-            first = PACK * n - share
-            for t in range(first // n + 1):
-                hi = min(first - t * n, n)
-                if hi > 0:
-                    gather_add(i, t, 0, hi)
-                if t + 1 == PAIR:
-                    store_sums(i, 0, PAIR, 0, n)
-            add_fetched(i)
-            store_sums(i, PAIR, PACK, 0, n)
-            round_columns(i, c0, c0 + n)
-        quantise(0)
-        store_words(0, STRETCH)
+        def round_run(r0, m, copy):
+            i = max(k for k, (c0, n) in enumerate(PIECES) if c0 <= r0)
+            lo = r0 - PIECES[i][0]
+            rounded[r0] = keep.tile([P, m, PACK], BF16, name=f"rounded{r0}", align_bytes=64)
+            copy(
+                rounded[r0][:].rearrange("p (c e) t -> p c t e", e=LINE),
+                summed[i][:, :, lo : lo + m].rearrange("p t (c e) -> p c t e", e=LINE),
+            )
 
-        i = len(PIECES) - 1
-        c0, n, share = PIECES[i]
-        cut = n - LAST
-        add_fetched(i)
-        store_sums(i, PAIR, PACK, 0, n)
-        for t in range(PAIR):
-            gather_add(i, t, 0, cut)
-            store_sums(i, t, t + 1, 0, cut)
-        round_columns(i, c0, c0 + cut)
-        quantise(1)
-        store_words(STRETCH, STRETCH)
-        for t in range(PAIR):
-            gather_add(i, t, cut, n)
-        store_sums(i, 0, PAIR, cut, n)
-        rounded.append(keep.tile([P, LAST, PACK], BF16, name="rounded_last", tag="summed1", align_bytes=64))
-        round_columns(i, c0 + cut, c0 + n)
-        for r in range(2, len(RUNS)):
-            quantise(r)
+        def quantise(r0, m, tag=None):
+            s, o = divmod(r0, STRETCH)
+            o_code[r0] = keep.tile([P, m], U32, name=f"o_code{r0}", tag=tag or f"o_code{r0}", align_bytes=64)
+            nc.vector.quantize_mx(
+                out=o_code[r0][:].bitcast(FP8X4),
+                scales=o_scale[PACK * s : P, o : o + m],
+                in_=rounded[r0][:].rearrange("p n t -> p (n t)"),
+            )
 
-        last_run, last_cols = RUNS[-1]
-        store_words(U - 2 * STRETCH, STRETCH)
-        store_words(U - STRETCH, STRETCH - last_cols)
+        def store_words(r0, m):
+            nc.sync.dma_start(words_out[:, PACK * r0 : PACK * (r0 + m)].bitcast(I32), o_code[r0][:].bitcast(I32))
+
+        lower = [(0, STRETCH)] + [(r0, RUN) for r0 in range(STRETCH, SPLIT, RUN)]
+        upper = [(r0, RUN) for r0 in range(SPLIT, U, RUN)]
+        for r0, m in lower:
+            round_run(r0, m, nc.scalar.copy)
+
+        def finish(run):
+            quantise(*run)
+            store_words(*run)
+
+        round_run(*upper[0], nc.vector.tensor_copy)
+        finish(lower[0])
+        round_run(*upper[1], nc.vector.tensor_copy)
+        finish(upper[0])
+        finish(lower[1])
+        round_run(*upper[2], nc.vector.tensor_copy)
+        finish(lower[2])
+        finish(upper[1])
+        finish(upper[2])
+        quantise(*lower[-1], tag=f"summed{PIECES[1][0]}")
 
         scales_out = out_2[0].rearrange("r (s c) -> s r c", c=STRETCH)
         for q in range(P // QUADRANT):
@@ -251,4 +222,4 @@ def tile_picked_unmerge_relu_po_kernel(tc, x_words, x_scales, w1, res, offs, own
                 scales_out[:, PACK * q : PACK * (q + 1), :].bitcast(I32),
                 o_scale[QUADRANT * q : QUADRANT * q + PACK * stretches, :].bitcast(I32),
             )
-        store_words(last_run, last_cols)
+        store_words(*lower[-1])

@@ -32,7 +32,8 @@ FIRST_PARTS = [(0, 256, False), (256, 256, False), (512, 256, False), (768, 128,
 OTHER_PARTS = [(0, BANK, False), (BANK, BANK, False)]
 PIECES = [(0, 768), (768, 768), (1536, 512)]
 RUN = 256
-SPLIT = 1280
+LOWER = [(0, 512), (512, 256), (768, 256), (1024, 128)]
+UPPER = [(1152, 384), (1536, 256), (1792, 256)]
 
 
 def tile_picked_unmerge_relu_po_kernel(tc, x_words, x_scales, w1, res, offs, own, out_0, out_1, out_2):
@@ -171,49 +172,45 @@ def tile_picked_unmerge_relu_po_kernel(tc, x_words, x_scales, w1, res, offs, own
         stretches = U // STRETCH
         o_scale = keep.tile([P, STRETCH], U8, name="o_scale", align_bytes=64)
         words_out = out_1[0].rearrange("p n j -> p (n j)")
-        rounded = {}
-        o_code = {}
 
-        def round_run(r0, m, copy):
-            i = max(k for k, (c0, n) in enumerate(PIECES) if c0 <= r0)
-            lo = r0 - PIECES[i][0]
-            rounded[r0] = keep.tile([P, m, PACK], BF16, name=f"rounded{r0}", align_bytes=64)
+        def round_columns(first, cols, copy):
+            i = max(k for k, (c0, n) in enumerate(PIECES) if c0 <= first)
+            lo = first - PIECES[i][0]
+            rounded = keep.tile([P, cols, PACK], BF16, name=f"rounded{first}", align_bytes=64)
             copy(
-                rounded[r0][:].rearrange("p (c e) t -> p c t e", e=LINE),
-                summed[i][:, :, lo : lo + m].rearrange("p t (c e) -> p c t e", e=LINE),
+                rounded[:].rearrange("p (c e) t -> p c t e", e=LINE),
+                summed[i][:, :, lo : lo + cols].rearrange("p t (c e) -> p c t e", e=LINE),
             )
+            return first, cols, rounded
 
-        def quantise(r0, m, tag=None):
-            s, o = divmod(r0, STRETCH)
-            o_code[r0] = keep.tile([P, m], U32, name=f"o_code{r0}", tag=tag or f"o_code{r0}", align_bytes=64)
-            nc.vector.quantize_mx(
-                out=o_code[r0][:].bitcast(FP8X4),
-                scales=o_scale[PACK * s : P, o : o + m],
-                in_=rounded[r0][:].rearrange("p n t -> p (n t)"),
-            )
+        def quantise(first, cols, rounded, tag=None):
+            codes = keep.tile([P, cols], U32, name=f"o_code{first}", tag=tag or f"o_code{first}", align_bytes=64)
+            lo = first
+            while lo < first + cols:
+                hi = first + cols if cols == STRETCH else min(first + cols, (lo // RUN + 1) * RUN)
+                s, o = divmod(lo, STRETCH)
+                nc.vector.quantize_mx(
+                    out=codes[:, lo - first : hi - first].bitcast(FP8X4),
+                    scales=o_scale[PACK * s : P, o : o + hi - lo],
+                    in_=rounded[:, lo - first : hi - first, :].rearrange("p n t -> p (n t)"),
+                )
+                lo = hi
+            return first, cols, codes
 
-        def store_words(r0, m):
-            nc.sync.dma_start(words_out[:, PACK * r0 : PACK * (r0 + m)].bitcast(I32), o_code[r0][:].bitcast(I32))
+        def store_words(first, cols, codes):
+            nc.sync.dma_start(words_out[:, PACK * first : PACK * (first + cols)].bitcast(I32), codes[:].bitcast(I32))
 
-        lower = [(0, STRETCH)] + [(r0, RUN) for r0 in range(STRETCH, SPLIT, RUN)]
-        upper = [(r0, RUN) for r0 in range(SPLIT, U, RUN)]
-        for r0, m in lower:
-            round_run(r0, m, nc.scalar.copy)
-
-        def finish(run):
-            quantise(*run)
-            store_words(*run)
-
-        round_run(*upper[0], nc.vector.tensor_copy)
-        finish(lower[0])
-        round_run(*upper[1], nc.vector.tensor_copy)
-        finish(upper[0])
-        finish(lower[1])
-        round_run(*upper[2], nc.vector.tensor_copy)
-        finish(lower[2])
-        finish(upper[1])
-        finish(upper[2])
-        quantise(*lower[-1], tag=f"summed{PIECES[1][0]}")
+        lower = [round_columns(first, cols, nc.scalar.copy) for first, cols in LOWER]
+        upper = [round_columns(*UPPER[0], nc.vector.tensor_copy)]
+        store_words(*quantise(*lower[0]))
+        upper.append(round_columns(*UPPER[1], nc.vector.tensor_copy))
+        store_words(*quantise(*upper[0]))
+        store_words(*quantise(*lower[1]))
+        upper.append(round_columns(*UPPER[2], nc.vector.tensor_copy))
+        store_words(*quantise(*lower[2]))
+        store_words(*quantise(*upper[1]))
+        store_words(*quantise(*upper[2]))
+        last = quantise(*lower[-1], tag=f"summed{PIECES[-1][0]}")
 
         scales_out = out_2[0].rearrange("r (s c) -> s r c", c=STRETCH)
         for q in range(P // QUADRANT):
@@ -222,4 +219,4 @@ def tile_picked_unmerge_relu_po_kernel(tc, x_words, x_scales, w1, res, offs, own
                 scales_out[:, PACK * q : PACK * (q + 1), :].bitcast(I32),
                 o_scale[QUADRANT * q : QUADRANT * q + PACK * stretches, :].bitcast(I32),
             )
-        store_words(*lower[-1])
+        store_words(*last)

@@ -28,12 +28,13 @@ STRETCH = 512
 FIRST_WORDS = 384
 EARLY = 768
 
-FIRST_PARTS = [(0, 256, False), (256, 256, False), (512, 256, False), (768, 128, True), (896, 128, False)]
+FIRST_PARTS = [(0, 256, False), (256, 256, False), (512, 256, True), (768, 128, True), (896, 128, False)]
+SECOND_PARTS = [(0, 256, False), (256, 256, False), (BANK, BANK, False)]
 OTHER_PARTS = [(0, BANK, False), (BANK, BANK, False)]
 PIECES = [(0, 768), (768, 768), (1536, 512)]
 RUN = 256
-LOWER = [(0, 512), (512, 256), (768, 256), (1024, 128)]
-UPPER = [(1152, 384), (1536, 256), (1792, 256)]
+BORDER = 448
+LAST = 128
 
 
 def tile_picked_unmerge_relu_po_kernel(tc, x_words, x_scales, w1, res, offs, own, out_0, out_1, out_2):
@@ -65,17 +66,17 @@ def tile_picked_unmerge_relu_po_kernel(tc, x_words, x_scales, w1, res, offs, own
 
         res_rows = res.rearrange("(p t) c -> p t c", t=PACK)
         out_rows = out_0.rearrange("(p t) c -> p t c", t=PACK)
-        first_cols = PIECES[0][1]
         res_sb = {}
         for t0 in range(0, PACK, PAIR):
-            for c0, n in ((0, first_cols), (first_cols, U - first_cols)):
+            cut = PIECES[1 if t0 == 0 else 2][0]
+            for c0, n in ((0, cut), (cut, U - cut)):
                 r = keep.tile([P, PAIR, n], F32, name=f"res{t0}_{c0}", align_bytes=64)
                 nc.sync.dma_start(r[:], res_rows[:, t0 : t0 + PAIR, c0 : c0 + n])
                 res_sb[t0, c0] = r
 
         def res_piece(i, t0):
             c0, n = PIECES[i]
-            start = min(c0, first_cols)
+            start = max(first for pair, first in res_sb if pair == t0 and first <= c0)
             return res_sb[t0, start][:, :, c0 - start : c0 - start + n]
 
         x_scale = keep.tile([P, S], U8, name="x_scale", align_bytes=64)
@@ -128,7 +129,7 @@ def tile_picked_unmerge_relu_po_kernel(tc, x_words, x_scales, w1, res, offs, own
         y = []
         for t in range(PACK):
             yt = keep.tile([P, S], F32, name=f"y{t}")
-            for e0, n, on_vector in FIRST_PARTS if t == 0 else OTHER_PARTS:
+            for e0, n, on_vector in [FIRST_PARTS, SECOND_PARTS, OTHER_PARTS, OTHER_PARTS][t]:
                 acc = psum.tile([P, n], F32, name="acc")
                 cut = min(n, EARLY - e0) if e0 < EARLY else n
                 product(acc[:, 0:cut], t, e0, cut)
@@ -150,67 +151,79 @@ def tile_picked_unmerge_relu_po_kernel(tc, x_words, x_scales, w1, res, offs, own
             for e in range(PAIR):
                 nc.scalar.activation(fetched[i][:, e, :], looked_up(i, PAIR + e), COPY)
 
-        def store_sums(i, t0):
+        def store_sums(i, t0, slots=PAIR):
             c0, n = PIECES[i]
-            nc.sync.dma_start(out_rows[:, t0 : t0 + PAIR, c0 : c0 + n], summed[i][:, t0 : t0 + PAIR, :])
+            nc.sync.dma_start(out_rows[:, t0 : t0 + slots, c0 : c0 + n], summed[i][:, t0 : t0 + slots, :])
 
         def gather_add(i):
             for t in range(PAIR):
                 nc.vector.tensor_tensor(summed[i][:, t, :], looked_up(i, t), res_piece(i, 0)[:, t, :], ADD)
-            store_sums(i, 0)
+                if i < 2:
+                    store_sums(i, t, 1)
+            if i == 2:
+                store_sums(i, 0)
 
         def add_fetched(i):
             nc.vector.tensor_tensor(summed[i][:, PAIR:PACK, :], fetched[i][:], res_piece(i, PAIR), ADD)
             store_sums(i, PAIR)
 
-        gather_add(0)
-        for i in range(1, len(PIECES)):
+        for i in range(len(PIECES)):
             gather_add(i)
-            add_fetched(i - 1)
-        add_fetched(len(PIECES) - 1)
+        for i in range(len(PIECES) - 1):
+            add_fetched(i)
 
         stretches = U // STRETCH
         o_scale = keep.tile([P, STRETCH], U8, name="o_scale", align_bytes=64)
         words_out = out_1[0].rearrange("p n j -> p (n j)")
 
-        def round_columns(first, cols, copy):
-            i = max(k for k, (c0, n) in enumerate(PIECES) if c0 <= first)
-            lo = first - PIECES[i][0]
-            rounded = keep.tile([P, cols, PACK], BF16, name=f"rounded{first}", align_bytes=64)
-            copy(
-                rounded[:].rearrange("p (c e) t -> p c t e", e=LINE),
-                summed[i][:, :, lo : lo + cols].rearrange("p t (c e) -> p c t e", e=LINE),
-            )
-            return first, cols, rounded
+        rounded = [keep.tile([P, n, PACK], BF16, name=f"rounded{c0}", align_bytes=64) for c0, n in PIECES]
 
-        def quantise(first, cols, rounded, tag=None):
-            codes = keep.tile([P, cols], U32, name=f"o_code{first}", tag=tag or f"o_code{first}", align_bytes=64)
-            lo = first
-            while lo < first + cols:
-                hi = first + cols if cols == STRETCH else min(first + cols, (lo // RUN + 1) * RUN)
-                s, o = divmod(lo, STRETCH)
-                nc.vector.quantize_mx(
-                    out=codes[:, lo - first : hi - first].bitcast(FP8X4),
-                    scales=o_scale[PACK * s : P, o : o + hi - lo],
-                    in_=rounded[:, lo - first : hi - first, :].rearrange("p n t -> p (n t)"),
-                )
-                lo = hi
-            return first, cols, codes
+        def in_piece(tiles, first):
+            i = max(k for k, (c0, n) in enumerate(PIECES) if c0 <= first)
+            return tiles[i], first - PIECES[i][0]
+
+        def round_columns(first, end, copy):
+            src, lo = in_piece(summed, first)
+            dst, lo = in_piece(rounded, first)
+            copy(
+                dst[:, lo : lo + end - first, :].rearrange("p (c e) t -> p c t e", e=LINE),
+                src[:, :, lo : lo + end - first].rearrange("p t (c e) -> p c t e", e=LINE),
+            )
+
+        def quantise(first, cols, codes):
+            src, lo = in_piece(rounded, first)
+            s, o = divmod(first, STRETCH)
+            nc.vector.quantize_mx(
+                out=codes.bitcast(FP8X4),
+                scales=o_scale[PACK * s : P, o : o + cols],
+                in_=src[:, lo : lo + cols, :].rearrange("p n t -> p (n t)"),
+            )
 
         def store_words(first, cols, codes):
-            nc.sync.dma_start(words_out[:, PACK * first : PACK * (first + cols)].bitcast(I32), codes[:].bitcast(I32))
+            nc.sync.dma_start(words_out[:, PACK * first : PACK * (first + cols)].bitcast(I32), codes.bitcast(I32))
 
-        lower = [round_columns(first, cols, nc.scalar.copy) for first, cols in LOWER]
-        upper = [round_columns(*UPPER[0], nc.vector.tensor_copy)]
-        store_words(*quantise(*lower[0]))
-        upper.append(round_columns(*UPPER[1], nc.vector.tensor_copy))
-        store_words(*quantise(*upper[0]))
-        store_words(*quantise(*lower[1]))
-        upper.append(round_columns(*UPPER[2], nc.vector.tensor_copy))
-        store_words(*quantise(*lower[2]))
-        store_words(*quantise(*upper[1]))
-        store_words(*quantise(*upper[2]))
-        last = quantise(*lower[-1], tag=f"summed{PIECES[-1][0]}")
+        def finish(first, cols, run):
+            codes = keep.tile([P, cols], U32, name=f"o_code{first}", align_bytes=64)
+            for lo in range(0, cols, run):
+                hi = min(lo + run, cols)
+                quantise(first + lo, hi - lo, codes[:, lo:hi])
+            store_words(first, cols, codes[:])
+
+        second, third = PIECES[1][0], PIECES[2][0]
+        round_columns(0, BORDER, nc.vector.tensor_copy)
+        add_fetched(len(PIECES) - 1)
+        round_columns(BORDER, second, nc.scalar.copy)
+        for first, end in ((second, second + RUN), (second + RUN, third - LAST), (third - LAST, third)):
+            round_columns(first, end, nc.scalar.copy)
+        finish(0, STRETCH, STRETCH)
+        round_columns(third, third + RUN, nc.vector.tensor_copy)
+        finish(STRETCH, STRETCH, RUN)
+        round_columns(third + RUN, U, nc.vector.tensor_copy)
+        finish(third, STRETCH, RUN)
+        finish(2 * STRETCH, STRETCH - LAST, RUN)
+        last_first, last_cols = third - LAST, LAST
+        last_code = keep.tile([P, last_cols], U32, name="last_code", tag=f"summed{second}", align_bytes=64)
+        quantise(last_first, last_cols, last_code[:])
 
         scales_out = out_2[0].rearrange("r (s c) -> s r c", c=STRETCH)
         for q in range(P // QUADRANT):
@@ -219,4 +232,4 @@ def tile_picked_unmerge_relu_po_kernel(tc, x_words, x_scales, w1, res, offs, own
                 scales_out[:, PACK * q : PACK * (q + 1), :].bitcast(I32),
                 o_scale[QUADRANT * q : QUADRANT * q + PACK * stretches, :].bitcast(I32),
             )
-        store_words(*last)
+        store_words(last_first, last_cols, last_code[:])

@@ -32,6 +32,8 @@ FIRST_PARTS = [(0, 256, False), (256, 256, False), (512, 256, True), (768, 128, 
 SECOND_PARTS = [(0, 256, False), (256, 256, False), (BANK, BANK, False)]
 OTHER_PARTS = [(0, BANK, False), (BANK, BANK, False)]
 PIECES = [(0, 768), (768, 768), (1536, 512)]
+SUMS = [(0, 0, 2), (1, 0, 2), (2, 0, 1), (0, 2, 2), (1, 2, 2), (2, 1, 1), (2, 2, 2)]
+RES_LOADS = [(0, 1, 0, 2), (1, 2, 0, 2), (2, 3, 0, 1), (0, 2, 2, 4), (2, 3, 1, 4)]
 RUN = 256
 BORDER = 448
 LAST = 128
@@ -67,17 +69,14 @@ def tile_picked_unmerge_relu_po_kernel(tc, x_words, x_scales, w1, res, offs, own
         res_rows = res.rearrange("(p t) c -> p t c", t=PACK)
         out_rows = out_0.rearrange("(p t) c -> p t c", t=PACK)
         res_sb = {}
-        for t0 in range(0, PACK, PAIR):
-            cut = PIECES[1 if t0 == 0 else 2][0]
-            for c0, n in ((0, cut), (cut, U - cut)):
-                r = keep.tile([P, PAIR, n], F32, name=f"res{t0}_{c0}", align_bytes=64)
-                nc.sync.dma_start(r[:], res_rows[:, t0 : t0 + PAIR, c0 : c0 + n])
-                res_sb[t0, c0] = r
-
-        def res_piece(i, t0):
-            c0, n = PIECES[i]
-            start = max(first for pair, first in res_sb if pair == t0 and first <= c0)
-            return res_sb[t0, start][:, :, c0 - start : c0 - start + n]
+        for i0, i1, t0, t1 in RES_LOADS:
+            c0, c1 = PIECES[i0][0], sum(PIECES[i1 - 1])
+            r = keep.tile([P, t1 - t0, c1 - c0], F32, name=f"res{i0}_{t0}", align_bytes=64)
+            nc.sync.dma_start(r[:], res_rows[:, t0:t1, c0:c1])
+            for i, first, slots in SUMS:
+                if i0 <= i < i1 and t0 <= first < t1:
+                    lo, n = PIECES[i][0] - c0, PIECES[i][1]
+                    res_sb[i, first] = r[:, first - t0 : first - t0 + slots, lo : lo + n]
 
         x_scale = keep.tile([P, S], U8, name="x_scale", align_bytes=64)
         early_code = keep.tile([P, EARLY], U32, name="early_code", align_bytes=64)
@@ -146,37 +145,36 @@ def tile_picked_unmerge_relu_po_kernel(tc, x_words, x_scales, w1, res, offs, own
             return y[t][:].indirect(own_sb[:, c0 // STRIPE : (c0 + n) // STRIPE])
 
         summed = [keep.tile([P, PACK, n], F32, name=f"summed{c0}", tag=f"summed{c0}", align_bytes=64) for c0, n in PIECES]
-        fetched = [keep.tile([P, PAIR, n], F32, name=f"fetched{c0}", align_bytes=64) for c0, n in PIECES]
+        fetched = [keep.tile([P, PAIR, n], F32, name=f"fetched{c0}", tag=f"fetched{c0}", align_bytes=64) for c0, n in PIECES]
         for i in range(len(PIECES)):
             for e in range(PAIR):
                 nc.scalar.activation(fetched[i][:, e, :], looked_up(i, PAIR + e), COPY)
 
-        def store_sums(i, t0, slots=PAIR):
+        def add_res(i, t0, slots):
             c0, n = PIECES[i]
-            nc.sync.dma_start(out_rows[:, t0 : t0 + slots, c0 : c0 + n], summed[i][:, t0 : t0 + slots, :])
+            out = summed[i][:, t0 : t0 + slots, :]
+            if t0 < PAIR:
+                for e in range(slots):
+                    nc.vector.tensor_tensor(out[:, e, :], looked_up(i, t0 + e), res_sb[i, t0][:, e, :], ADD)
+            elif i == 1:
+                for e in range(slots):
+                    nc.vector.tensor_tensor(out[:, e, :], fetched[i][:, e, :], res_sb[i, t0][:, e, :], ADD)
+            else:
+                nc.vector.tensor_tensor(out, fetched[i][:], res_sb[i, t0], ADD)
+            nc.sync.dma_start(out_rows[:, t0 : t0 + slots, c0 : c0 + n], out)
 
-        def gather_add(i):
-            for t in range(PAIR):
-                nc.vector.tensor_tensor(summed[i][:, t, :], looked_up(i, t), res_piece(i, 0)[:, t, :], ADD)
-                if i < 2:
-                    store_sums(i, t, 1)
-            if i == 2:
-                store_sums(i, 0)
-
-        def add_fetched(i):
-            nc.vector.tensor_tensor(summed[i][:, PAIR:PACK, :], fetched[i][:], res_piece(i, PAIR), ADD)
-            store_sums(i, PAIR)
-
-        for i in range(len(PIECES)):
-            gather_add(i)
-        for i in range(len(PIECES) - 1):
-            add_fetched(i)
+        for part in SUMS[:-1]:
+            add_res(*part)
 
         stretches = U // STRETCH
         o_scale = keep.tile([P, STRETCH], U8, name="o_scale", align_bytes=64)
         words_out = out_1[0].rearrange("p n j -> p (n j)")
 
-        rounded = [keep.tile([P, n, PACK], BF16, name=f"rounded{c0}", align_bytes=64) for c0, n in PIECES]
+        tags = [f"fetched{PIECES[1][0]}"] + [f"rounded{c0}" for c0, n in PIECES[1:]]
+        rounded = [
+            keep.tile([P, n, PACK], BF16, name=f"rounded{c0}", tag=tag, align_bytes=64)
+            for (c0, n), tag in zip(PIECES, tags)
+        ]
 
         def in_piece(tiles, first):
             i = max(k for k, (c0, n) in enumerate(PIECES) if c0 <= first)
@@ -211,7 +209,7 @@ def tile_picked_unmerge_relu_po_kernel(tc, x_words, x_scales, w1, res, offs, own
 
         second, third = PIECES[1][0], PIECES[2][0]
         round_columns(0, BORDER, nc.vector.tensor_copy)
-        add_fetched(len(PIECES) - 1)
+        add_res(*SUMS[-1])
         round_columns(BORDER, second, nc.scalar.copy)
         for first, end in ((second, second + RUN), (second + RUN, third - LAST), (third - LAST, third)):
             round_columns(first, end, nc.scalar.copy)

@@ -36,7 +36,6 @@ SUMS = [(0, 0, 2), (1, 0, 2), (2, 0, 1), (0, 2, 2), (1, 2, 2), (2, 1, 1), (2, 2,
 RES_LOADS = [(0, 1, 0, 2), (1, 2, 0, 2), (2, 3, 0, 1), (0, 2, 2, 4), (2, 3, 1, 4)]
 RUN = 256
 BORDER = 448
-LAST = 128
 
 
 def tile_picked_unmerge_relu_po_kernel(tc, x_words, x_scales, w1, res, offs, own, out_0, out_1, out_2):
@@ -200,26 +199,26 @@ def tile_picked_unmerge_relu_po_kernel(tc, x_words, x_scales, w1, res, offs, own
         def store_words(first, cols, codes):
             nc.sync.dma_start(words_out[:, PACK * first : PACK * (first + cols)].bitcast(I32), codes.bitcast(I32))
 
-        def finish(first, cols, run):
+        def finish(first, *runs):
+            cols = sum(n for lo, n in runs)
             codes = keep.tile([P, cols], U32, name=f"o_code{first}", align_bytes=64)
-            for lo in range(0, cols, run):
-                hi = min(lo + run, cols)
-                quantise(first + lo, hi - lo, codes[:, lo:hi])
+            for lo, n in runs:
+                quantise(lo, n, codes[:, lo - first : lo - first + n])
             store_words(first, cols, codes[:])
 
         second, third = PIECES[1][0], PIECES[2][0]
         round_columns(0, BORDER, nc.vector.tensor_copy)
         add_res(*SUMS[-1])
         round_columns(BORDER, second, nc.scalar.copy)
-        for first, end in ((second, second + RUN), (second + RUN, third - LAST), (third - LAST, third)):
-            round_columns(first, end, nc.scalar.copy)
-        finish(0, STRETCH, STRETCH)
+        for first in (second, third - RUN, second + RUN):
+            round_columns(first, first + RUN, nc.scalar.copy)
+        finish(0, (0, STRETCH))
         round_columns(third, third + RUN, nc.vector.tensor_copy)
-        finish(STRETCH, STRETCH, RUN)
+        finish(STRETCH, (STRETCH, RUN), (second, RUN))
+        finish(third - RUN, (third, RUN), (third - RUN, RUN))
         round_columns(third + RUN, U, nc.vector.tensor_copy)
-        finish(third, STRETCH, RUN)
-        finish(2 * STRETCH, STRETCH - LAST, RUN)
-        last_first, last_cols = third - LAST, LAST
+        finish(second + RUN, (second + RUN, RUN))
+        last_first, last_cols = U - RUN, RUN
         last_code = keep.tile([P, last_cols], U32, name="last_code", tag=f"summed{second}", align_bytes=64)
         quantise(last_first, last_cols, last_code[:])
 

@@ -28,11 +28,11 @@ STRETCH = 512
 FIRST_WORDS = 384
 EARLY = 768
 
-FIRST_PARTS = [(0, 256, False), (256, 256, False), (512, 256, True), (768, 128, True), (896, 128, False)]
+FIRST_PARTS = [(0, 256, False), (256, 256, False), (512, 256, False), (768, 128, True), (896, 64, True), (960, 64, False)]
 SECOND_PARTS = [(0, 256, False), (256, 256, False), (BANK, BANK, False)]
 OTHER_PARTS = [(0, BANK, False), (BANK, BANK, False)]
 PIECES = [(0, 768), (768, 768), (1536, 512)]
-SUMS = [(0, 0, 2), (1, 0, 2), (2, 0, 1), (0, 2, 2), (1, 2, 2), (2, 1, 1), (2, 2, 2)]
+SUMS = [(0, 0, 2), (1, 0, 2), (2, 0, 1), (0, 2, 2), (1, 2, 2), (2, 1, 2), (2, 3, 1)]
 RES_LOADS = [(0, 1, 0, 2), (1, 2, 0, 2), (2, 3, 0, 1), (0, 2, 2, 4), (2, 3, 1, 4)]
 RUN = 256
 BORDER = 448
@@ -97,17 +97,17 @@ def tile_picked_unmerge_relu_po_kernel(tc, x_words, x_scales, w1, res, offs, own
             nc.scalar.copy(w_rest[:].rearrange("p t m j -> p m j t")[:, :, js, :], src[:, :, :, 1:PACK])
         w_code = []
         w_scale = []
-        for t in range(PACK):
-            codes = keep.tile([P, P], U32, name=f"w_code{t}", align_bytes=64)
-            scales = keep.tile([P, P], U8, name=f"w_scale{t}", align_bytes=64)
-            w_bf = w_first[:, 0, :, :] if t == 0 else w_rest[:, t - 1, :, :]
+        for t, slots in ((0, 1), (1, 1), (PAIR, PAIR)):
+            codes = keep.tile([P, slots * P], U32, name=f"w_code{t}", align_bytes=64)
+            scales = keep.tile([P, slots * P], U8, name=f"w_scale{t}", align_bytes=64)
+            w_bf = w_first[:] if t == 0 else w_rest[:, t - 1 : t - 1 + slots, :, :]
             nc.vector.quantize_mx(
                 out=codes[:].bitcast(FP8X4),
                 scales=scales[:],
-                in_=w_bf.rearrange("p m j -> p (m j)"),
+                in_=w_bf.rearrange("p t m j -> p (t m j)"),
             )
-            w_code.append(codes)
-            w_scale.append(scales)
+            w_code.extend(codes[:, e * P : (e + 1) * P] for e in range(slots))
+            w_scale.extend(scales[:, e * P : (e + 1) * P] for e in range(slots))
             if t == 0:
                 late_code = keep.tile([P, S - EARLY], U32, name="late_code", tag="first", align_bytes=64)
                 nc.vector.tensor_copy(late_code[:], words.indirect(offs_sb[:, EARLY // STRIPE : S // STRIPE]))
@@ -116,8 +116,8 @@ def tile_picked_unmerge_relu_po_kernel(tc, x_words, x_scales, w1, res, offs, own
             x_code = early_code[:, e0 : e0 + n] if e0 < EARLY else late_code[:, e0 - EARLY : e0 - EARLY + n]
             nc.tensor.matmul_mx(
                 out=out,
-                lhsT=w_code[t][:].bitcast(FP8X4),
-                lhsT_scale=w_scale[t][:],
+                lhsT=w_code[t].bitcast(FP8X4),
+                lhsT_scale=w_scale[t],
                 rhs=x_code.bitcast(FP8X4),
                 rhs_scale=x_scale[:, e0 : e0 + n],
                 start=True,
@@ -152,14 +152,13 @@ def tile_picked_unmerge_relu_po_kernel(tc, x_words, x_scales, w1, res, offs, own
         def add_res(i, t0, slots):
             c0, n = PIECES[i]
             out = summed[i][:, t0 : t0 + slots, :]
-            if t0 < PAIR:
-                for e in range(slots):
-                    nc.vector.tensor_tensor(out[:, e, :], looked_up(i, t0 + e), res_sb[i, t0][:, e, :], ADD)
-            elif i == 1:
-                for e in range(slots):
-                    nc.vector.tensor_tensor(out[:, e, :], fetched[i][:, e, :], res_sb[i, t0][:, e, :], ADD)
-            else:
+            if (i, t0) == (0, PAIR):
                 nc.vector.tensor_tensor(out, fetched[i][:], res_sb[i, t0], ADD)
+            else:
+                for e in range(slots):
+                    t = t0 + e
+                    values = looked_up(i, t) if t < PAIR else fetched[i][:, t - PAIR, :]
+                    nc.vector.tensor_tensor(out[:, e, :], values, res_sb[i, t0][:, e, :], ADD)
             nc.sync.dma_start(out_rows[:, t0 : t0 + slots, c0 : c0 + n], out)
 
         for part in SUMS[:-1]:

from contextlib import ExitStack

import concourse.mybir as mybir

K, T, S, N, U = 512, 2048, 1024, 512, 2048
FLOPS = 2 * K * N * S

F32 = mybir.dt.float32
BF16 = mybir.dt.bfloat16
I32 = mybir.dt.int32
U32 = mybir.dt.uint32
U16 = mybir.dt.uint16
U8 = mybir.dt.uint8
FP8X4 = mybir.dt.float8_e4m3fn_x4
ADD = mybir.AluOpType.add
RELU = mybir.ActivationFunctionType.Relu
COPY = mybir.ActivationFunctionType.Copy

P = 128
PACK = 4
PAIR = 2
QUADRANT = 32
BANK = 512
BANKS = 8
STRIPE = 16
LINE = 4
STRETCH = 512
FIRST_WORDS = 384
EARLY = 768

FIRST_PARTS = [(0, 256, False), (256, 256, False), (512, 256, False), (768, 128, True), (896, 64, True), (960, 64, False)]
SECOND_PARTS = [(0, 256, False), (256, 256, False), (BANK, BANK, False)]
OTHER_PARTS = [(0, BANK, False), (BANK, BANK, False)]
PIECES = [(0, 768), (768, 768), (1536, 512)]
SUMS = [(0, 0, 2), (1, 0, 2), (2, 0, 1), (0, 2, 2), (1, 2, 2), (2, 1, 2), (2, 3, 1)]
RES_LOADS = [(0, 1, 0, 2), (1, 2, 0, 2), (2, 3, 0, 1), (0, 2, 2, 4), (2, 3, 1, 4)]
RUN = 256
BORDER = 448


def tile_picked_unmerge_relu_po_kernel(tc, x_words, x_scales, w1, res, offs, own, out_0, out_1, out_2):
    nc = tc.nc
    with ExitStack() as ctx:
        keep = ctx.enter_context(tc.tile_pool(name="keep", bufs=1))
        psum = ctx.enter_context(tc.psum_pool(name="psum", bufs=BANKS))

        offs_sb = keep.tile([P, S // STRIPE], U16, name="offs_sb")
        own_sb = keep.tile([P, U // STRIPE], U16, name="own_sb")
        scale_table = keep.tile([P, T], U8, name="scale_table", align_bytes=64)
        word_table = keep.tile([P, T], I32, name="word_table", align_bytes=64)
        w_raw = [keep.tile([P, PAIR, N], F32, name=f"w_raw{j0}") for j0 in range(0, PACK, PAIR)]

        nc.vector.memset(scale_table[:].bitcast(I32), 0)
        nc.sync.dma_start(offs_sb[:], offs)
        words_in = x_words[0].rearrange("p n j -> p (n j)").bitcast(I32)
        nc.sync.dma_start(word_table[:, 0:FIRST_WORDS], words_in[:, 0:FIRST_WORDS])
        scale_rows = x_scales[0].rearrange("(q r) c -> r q c", r=PACK)
        for r in range(PACK):
            queue = nc.sync if r % 2 == 0 else nc.scalar
            queue.dma_start(scale_table[r:P:QUADRANT, :].bitcast(I32), scale_rows[r].bitcast(I32))
        w_rows = w1.rearrange("(p j) c -> p j c", j=PACK)
        nc.sync.dma_start(w_raw[0][:], w_rows[:, 0:PAIR, :])
        nc.sync.dma_start(word_table[:, FIRST_WORDS:T], words_in[:, FIRST_WORDS:T])
        for e in range(PAIR):
            nc.sync.dma_start(w_raw[1][:, e, :], w_rows[:, PAIR + e, :])
        nc.sync.dma_start(own_sb[:], own)

        res_rows = res.rearrange("(p t) c -> p t c", t=PACK)
        out_rows = out_0.rearrange("(p t) c -> p t c", t=PACK)
        res_sb = {}
        for i0, i1, t0, t1 in RES_LOADS:
            c0, c1 = PIECES[i0][0], sum(PIECES[i1 - 1])
            r = keep.tile([P, t1 - t0, c1 - c0], F32, name=f"res{i0}_{t0}", align_bytes=64)
            nc.sync.dma_start(r[:], res_rows[:, t0:t1, c0:c1])
            for i, first, slots in SUMS:
                if i0 <= i < i1 and t0 <= first < t1:
                    lo, n = PIECES[i][0] - c0, PIECES[i][1]
                    res_sb[i, first] = r[:, first - t0 : first - t0 + slots, lo : lo + n]

        x_scale = keep.tile([P, S], U8, name="x_scale", align_bytes=64)
        early_code = keep.tile([P, EARLY], U32, name="early_code", align_bytes=64)
        words = word_table[:].bitcast(U32)
        nc.vector.tensor_copy(x_scale[:], scale_table[:].indirect(offs_sb[:]))
        nc.vector.tensor_copy(early_code[:], words.indirect(offs_sb[:, 0 : EARLY // STRIPE]))

        w_src = [raw[:].rearrange("p j (m t) -> p m j t", t=PACK) for raw in w_raw]
        w_first = keep.tile([P, 1, P, PACK], BF16, name="w_first", tag="first", align_bytes=64)
        w_rest = keep.tile([P, PACK - 1, P, PACK], BF16, name="w_rest", align_bytes=64)
        for v, src in enumerate(w_src):
            js = slice(v * PAIR, (v + 1) * PAIR)
            rows = PAIR if v == 0 else 1
            for e in range(0, PAIR, rows):
                nc.scalar.copy(
                    w_first[:].rearrange("p t m j -> p m j t")[:, :, v * PAIR + e : v * PAIR + e + rows, :],
                    src[:, :, e : e + rows, 0:1],
                )
            nc.scalar.copy(w_rest[:].rearrange("p t m j -> p m j t")[:, :, js, :], src[:, :, :, 1:PACK])
        w_code = []
        w_scale = []
        for t, slots in ((0, 1), (1, 1), (PAIR, PAIR)):
            codes = keep.tile([P, slots * P], U32, name=f"w_code{t}", align_bytes=64)
            scales = keep.tile([P, slots * P], U8, name=f"w_scale{t}", align_bytes=64)
            w_bf = w_first[:] if t == 0 else w_rest[:, t - 1 : t - 1 + slots, :, :]
            nc.vector.quantize_mx(
                out=codes[:].bitcast(FP8X4),
                scales=scales[:],
                in_=w_bf.rearrange("p t m j -> p (t m j)"),
            )
            w_code.extend(codes[:, e * P : (e + 1) * P] for e in range(slots))
            w_scale.extend(scales[:, e * P : (e + 1) * P] for e in range(slots))
            if t == 0:
                late_code = keep.tile([P, S - EARLY], U32, name="late_code", tag="first", align_bytes=64)
                nc.vector.tensor_copy(late_code[:], words.indirect(offs_sb[:, EARLY // STRIPE : S // STRIPE]))

        def product(out, t, e0, n):
            x_code = early_code[:, e0 : e0 + n] if e0 < EARLY else late_code[:, e0 - EARLY : e0 - EARLY + n]
            nc.tensor.matmul_mx(
                out=out,
                lhsT=w_code[t].bitcast(FP8X4),
                lhsT_scale=w_scale[t],
                rhs=x_code.bitcast(FP8X4),
                rhs_scale=x_scale[:, e0 : e0 + n],
                start=True,
                stop=True,
            )

        y = []
        for t in range(PACK):
            yt = keep.tile([P, S], F32, name=f"y{t}")
            for e0, n, on_vector in [FIRST_PARTS, SECOND_PARTS, OTHER_PARTS, OTHER_PARTS][t]:
                acc = psum.tile([P, n], F32, name="acc")
                cut = min(n, EARLY - e0) if e0 < EARLY else n
                product(acc[:, 0:cut], t, e0, cut)
                if cut < n:
                    product(acc[:, cut:n], t, e0 + cut, n - cut)
                if on_vector:
                    nc.vector.tensor_scalar_max(yt[:, e0 : e0 + n], acc[:], 0.0)
                else:
                    nc.scalar.activation(yt[:, e0 : e0 + n], acc[:], RELU)
            y.append(yt)

        def looked_up(i, t):
            c0, n = PIECES[i]
            return y[t][:].indirect(own_sb[:, c0 // STRIPE : (c0 + n) // STRIPE])

        summed = [keep.tile([P, PACK, n], F32, name=f"summed{c0}", tag=f"summed{c0}", align_bytes=64) for c0, n in PIECES]
        fetched = [keep.tile([P, PAIR, n], F32, name=f"fetched{c0}", tag=f"fetched{c0}", align_bytes=64) for c0, n in PIECES]
        for i in range(len(PIECES)):
            for e in range(PAIR):
                nc.scalar.activation(fetched[i][:, e, :], looked_up(i, PAIR + e), COPY)

        def add_res(i, t0, slots):
            c0, n = PIECES[i]
            out = summed[i][:, t0 : t0 + slots, :]
            if (i, t0) == (0, PAIR):
                nc.vector.tensor_tensor(out, fetched[i][:], res_sb[i, t0], ADD)
            else:
                for e in range(slots):
                    t = t0 + e
                    values = looked_up(i, t) if t < PAIR else fetched[i][:, t - PAIR, :]
                    nc.vector.tensor_tensor(out[:, e, :], values, res_sb[i, t0][:, e, :], ADD)
            nc.sync.dma_start(out_rows[:, t0 : t0 + slots, c0 : c0 + n], out)

        for part in SUMS[:-1]:
            add_res(*part)

        stretches = U // STRETCH
        o_scale = keep.tile([P, STRETCH], U8, name="o_scale", align_bytes=64)
        words_out = out_1[0].rearrange("p n j -> p (n j)")

        tags = [f"fetched{PIECES[1][0]}"] + [f"rounded{c0}" for c0, n in PIECES[1:]]
        rounded = [
            keep.tile([P, n, PACK], BF16, name=f"rounded{c0}", tag=tag, align_bytes=64)
            for (c0, n), tag in zip(PIECES, tags)
        ]

        def in_piece(tiles, first):
            i = max(k for k, (c0, n) in enumerate(PIECES) if c0 <= first)
            return tiles[i], first - PIECES[i][0]

        def round_columns(first, end, copy):
            src, lo = in_piece(summed, first)
            dst, lo = in_piece(rounded, first)
            copy(
                dst[:, lo : lo + end - first, :].rearrange("p (c e) t -> p c t e", e=LINE),
                src[:, :, lo : lo + end - first].rearrange("p t (c e) -> p c t e", e=LINE),
            )

        def quantise(first, cols, codes):
            src, lo = in_piece(rounded, first)
            s, o = divmod(first, STRETCH)
            nc.vector.quantize_mx(
                out=codes.bitcast(FP8X4),
                scales=o_scale[PACK * s : P, o : o + cols],
                in_=src[:, lo : lo + cols, :].rearrange("p n t -> p (n t)"),
            )

        def store_words(first, cols, codes):
            nc.sync.dma_start(words_out[:, PACK * first : PACK * (first + cols)].bitcast(I32), codes.bitcast(I32))

        def finish(first, *runs):
            cols = sum(n for lo, n in runs)
            codes = keep.tile([P, cols], U32, name=f"o_code{first}", align_bytes=64)
            for lo, n in runs:
                quantise(lo, n, codes[:, lo - first : lo - first + n])
            store_words(first, cols, codes[:])

        second, third = PIECES[1][0], PIECES[2][0]
        round_columns(0, BORDER, nc.vector.tensor_copy)
        add_res(*SUMS[-1])
        round_columns(BORDER, second, nc.scalar.copy)
        for first in (second, third - RUN, second + RUN):
            round_columns(first, first + RUN, nc.scalar.copy)
        finish(0, (0, STRETCH))
        round_columns(third, third + RUN, nc.vector.tensor_copy)
        finish(STRETCH, (STRETCH, RUN), (second, RUN))
        finish(third - RUN, (third, RUN), (third - RUN, RUN))
        round_columns(third + RUN, U, nc.vector.tensor_copy)
        finish(second + RUN, (second + RUN, RUN))
        last_first, last_cols = U - RUN, RUN
        last_code = keep.tile([P, last_cols], U32, name="last_code", tag=f"summed{second}", align_bytes=64)
        quantise(last_first, last_cols, last_code[:])

        scales_out = out_2[0].rearrange("r (s c) -> s r c", c=STRETCH)
        for q in range(P // QUADRANT):
            queue = nc.sync if q % 2 == 0 else nc.scalar
            queue.dma_start(
                scales_out[:, PACK * q : PACK * (q + 1), :].bitcast(I32),
                o_scale[QUADRANT * q : QUADRANT * q + PACK * stretches, :].bitcast(I32),
            )
        store_words(last_first, last_cols, last_code[:])
